import numpy as np
import ml_dtypes


def mxq(x, axis, fmt="e4m3"):
    dtype, down = {"e4m3": (ml_dtypes.float8_e4m3fn, 7), "e5m2": (ml_dtypes.float8_e5m2, 14)}[fmt]
    v = np.moveaxis(np.asarray(x, np.float32).astype(ml_dtypes.bfloat16).astype(np.float64), axis, -1)
    blocks = v.reshape(v.shape[:-1] + (-1, 32))
    amax = np.abs(blocks).max(-1, keepdims=True)
    byte = np.maximum(np.where(amax > 0, np.frexp(amax)[1] - 1 + 127, 0) - down, 1)
    scale = np.exp2(byte - 127.0)
    codes = (blocks / scale).astype(np.float32).astype(dtype).astype(np.float64)
    return np.moveaxis((codes * scale).reshape(v.shape), -1, axis)


WIDE = False


def mx_kscale(k):
    if not WIDE:
        return np.ones(k)
    levels = np.array([10, -10, 5, -5, 0])
    if k % 512:
        return np.exp2(np.random.permutation(np.resize(levels, k // 32))).repeat(32)
    a = np.empty((k // 512, 16))
    for p in range(k // 512):
        a[p, :8] = np.random.permutation(np.resize(levels, 8))
        for g in range(8):
            far = levels[np.abs(levels - a[p, g]) >= 10]
            a[p, g + 8] = far[np.random.randint(len(far))]
    return np.exp2(a.ravel()).repeat(32)


def f64(x):
    return np.asarray(x).astype(np.float64)


def striped(idx):
    return np.tile(np.asarray(idx).reshape(-1, 16).T, (8, 1)).astype(np.uint16)


def unstriped(offs):
    return offs[:16].T.reshape(-1).astype(np.int64)


def striped8(idx):
    return np.asarray(idx).reshape(8, -1, 16).transpose(0, 2, 1).reshape(128, -1).astype(np.uint16)


def unstriped8(offs):
    return offs.reshape(8, 16, -1).transpose(0, 2, 1).reshape(8, -1).astype(np.int64)


def pick8(x, idx, run):
    r = np.arange(len(x))
    return x[r[:, None], idx[r % (8 * run) // run]]


E2M1 = np.array([0.0, 0.5, 1.0, 1.5, 2.0, 3.0, 4.0, 6.0, -0.0, -0.5, -1.0, -1.5, -2.0, -3.0, -4.0, -6.0])


def pack_weight(w, fmt):
    k, n = w.shape
    w = f64(np.asarray(w, np.float32).astype(ml_dtypes.bfloat16)).reshape(k // 32, 32, n)
    amax = np.abs(w).max(1)
    if fmt == "e4m3":
        byte = np.frexp(amax)[1] - 1 + 127 - 7
    else:
        mant, ex = np.frexp(amax / 6.0)
        byte = np.where(mant > 0.5, ex, ex - 1) + 127
    byte = np.clip(np.where(amax > 0, byte, 1), 1, 254)
    scaled = (w * np.exp2(127.0 - byte)[:, None, :]).reshape(k, n).astype(np.float32)
    by_word = np.ascontiguousarray(scaled.reshape(k // 512, 128, 4, n).transpose(0, 1, 3, 2))
    if fmt == "e4m3":
        words = by_word.astype(ml_dtypes.float8_e4m3fn).view(np.uint8)
    else:
        c = by_word.astype(ml_dtypes.float4_e2m1fn).view(np.uint8) & 0xF
        words = (c[..., 0::2] | (c[..., 1::2] << 4)).reshape(k // 512, 128, 2 * n)
    return np.ascontiguousarray(words), np.ascontiguousarray(byte.astype(np.uint8).reshape(k // 512, 16, n))


def unpack_weight(words, scales, fmt):
    g, _, n = scales.shape
    words = np.ascontiguousarray(words).reshape(g, 128, n, -1)
    if fmt == "e4m3":
        vals = words.view(ml_dtypes.float8_e4m3fn).astype(np.float64)
    else:
        nib = np.empty((g, 128, n, 4), np.uint8)
        nib[..., 0::2] = words & 0xF
        nib[..., 1::2] = words >> 4
        vals = E2M1[nib]
    vals = vals * np.repeat(np.exp2(scales.astype(np.float64) - 127.0), 8, axis=1)[..., None]
    return vals.transpose(0, 1, 3, 2).reshape(g * 512, n)


K, U, I, T, E, F = 512, 2048, 256, 512, 512, 512


def setup_inputs():
    n = np.random.standard_normal
    idx = np.random.permutation(U)[:I]
    idx2 = np.stack([np.random.permutation(T)[:I] for _ in range(8)])
    fk = mx_kscale(K)
    fe = mx_kscale(E)
    embp = pack_weight(n((K, U)) / fk[:, None], "e2m1")
    return {
        "emb_words": embp[0],
        "emb_scales": embp[1],
        "wv": (n((K, E)) * 1 / np.sqrt(K) * fk[:, None] * fe).astype(np.float32),
        "base": (n((E, T)) * fe[:, None]).astype(np.float32),
        "wo": (n((E, F)) * 1 / np.sqrt(E) / fe[:, None]).astype(np.float32),
        "offs": striped(idx),
        "offs2": striped8(idx2),
    }


def reference(emb_words, emb_scales, wv, base, wo, offs, offs2):
    idx = unstriped(offs)
    idx2 = unstriped8(offs2)
    embu = unpack_weight(emb_words, emb_scales, "e2m1")
    wvq = mxq(f64(wv), 0, "e4m3")
    embidxg = embu[:, idx]
    v = wvq.T @ embidxg
    vf = np.zeros((E, T))
    vf[np.arange(E)[:, None], idx2[np.arange(E) % 512 // 64]] = v
    x = vf + f64(base)
    woq = mxq(f64(wo), 0, "e4m3")
    xq = mxq(x, 0, "e4m3")
    y = woq.T @ xq
    return y

@@ -1,0 +1,133 @@
+from contextlib import ExitStack
+
+import concourse.mybir as mybir
+
+K, U, I, T, E, F = 512, 2048, 256, 512, 512, 512
+FLOPS = 2 * K * E * I + 2 * E * F * T
+
+F32 = mybir.dt.float32
+BF16 = mybir.dt.bfloat16
+I32 = mybir.dt.int32
+U32 = mybir.dt.uint32
+U16 = mybir.dt.uint16
+U8 = mybir.dt.uint8
+FP8X4 = mybir.dt.float8_e4m3fn_x4
+FP4X4 = mybir.dt.float4_e2m1fn_x4
+ADD = mybir.AluOpType.add
+
+P = 128
+PACK = 4
+HALVES = 2
+M_HALF = P // HALVES
+M_VECTOR = 40
+CHUNKS = 4
+TC = T // CHUNKS
+
+
+def tile_attend_headpage_proj_kernel(tc, emb_words, emb_scales, wv, base, wo, offs, offs2, out):
+    nc = tc.nc
+    with ExitStack() as ctx:
+        keep = ctx.enter_context(tc.tile_pool(name="keep", bufs=1))
+        psum = ctx.enter_context(tc.psum_pool(name="psum", bufs=1))
+
+        offs_sb = keep.tile([P, I // 16], U16, name="offs_sb")
+        offs2_sb = keep.tile([P, I // 16], U16, name="offs2_sb")
+        words = keep.tile([P, U], U16, name="words", align_bytes=64)
+        scales = keep.tile([P, U], U8, name="scales", align_bytes=64)
+        wv_raw = [keep.tile([P, PACK, E // HALVES], F32, name="wv_raw%d" % h, align_bytes=64) for h in range(HALVES)]
+        base_sb = keep.tile([P, PACK, T], F32, name="base_sb", align_bytes=64)
+        wo_raw = keep.tile([P, PACK, F], F32, name="wo_raw", align_bytes=64)
+        page = [keep.tile([P, T], F32, name="page%d" % j, align_bytes=64) for j in range(PACK)]
+
+        nc.vector.memset(scales[:].bitcast(I32), 0)
+        nc.sync.dma_start(offs_sb[:], offs)
+        wv_rows = wv.rearrange("(p j) e -> p j e", j=PACK)
+        for h in range(HALVES):
+            nc.sync.dma_start(wv_raw[h][:], wv_rows[:, :, h * (E // HALVES) : (h + 1) * (E // HALVES)])
+        nc.sync.dma_start(words[:].bitcast(I32), emb_words[0].bitcast(I32))
+        for q in range(4):
+            nc.scalar.dma_start(scales[32 * q : 32 * q + 4, :].bitcast(I32), emb_scales[0, 4 * q : 4 * q + 4, :].bitcast(I32))
+        nc.sync.dma_start(offs2_sb[:], offs2)
+        nc.sync.dma_start(base_sb[:], base.rearrange("(p j) t -> p j t", j=PACK))
+        nc.sync.dma_start(wo_raw[:], wo.rearrange("(p j) f -> p j f", j=PACK))
+        for j in range(PACK):
+            nc.vector.memset(page[j][:], 0.0)
+
+        got_scales = keep.tile([P, I], U8, name="got_scales", align_bytes=64)
+        nc.vector.tensor_copy(got_scales[:], scales[:].indirect(offs_sb[:]))
+
+        wv_bf = keep.tile([P, PACK, P, PACK], BF16, name="wv_bf", align_bytes=64)
+        for h in range(HALVES):
+            src = wv_raw[h][:].rearrange("p j (m t) -> p m t j", t=PACK)
+            dst = wv_bf[:, :, h * M_HALF : (h + 1) * M_HALF, :].rearrange("p t m j -> p m t j")
+            nc.scalar.copy(dst[:, M_VECTOR:], src[:, M_VECTOR:])
+            nc.vector.tensor_copy(dst[:, :M_VECTOR], src[:, :M_VECTOR])
+        wv_codes = keep.tile([P, E], U32, name="wv_codes", align_bytes=64)
+        wv_scales = keep.tile([P, E], U8, name="wv_scales", align_bytes=64)
+        for j in range(PACK):
+            cols = slice(j * P, (j + 1) * P)
+            nc.vector.quantize_mx(out=wv_codes[:, cols].bitcast(FP8X4), scales=wv_scales[:, cols],
+                                  in_=wv_bf[:, j].rearrange("p m j -> p (m j)"))
+
+        got_words = keep.tile([P, I], U16, name="got_words", align_bytes=64)
+        nc.vector.tensor_copy(got_words[:], words[:].indirect(offs_sb[:]))
+
+        v_sb = [keep.tile([P, I], F32, name="v_sb%d" % j, align_bytes=64) for j in range(PACK)]
+        for j in range(PACK):
+            cols = slice(j * P, (j + 1) * P)
+            v_ps = psum.tile([P, I], F32, name="v_ps%d" % j)
+            nc.tensor.matmul_mx(out=v_ps[:], lhsT=wv_codes[:, cols].bitcast(FP8X4), lhsT_scale=wv_scales[:, cols],
+                                rhs=got_words[:].bitcast(FP4X4), rhs_scale=got_scales[:], start=True, stop=True)
+            nc.scalar.copy(v_sb[j][:], v_ps[:])
+
+        wo_bf = keep.tile([P, F, PACK], BF16, name="wo_bf", align_bytes=64)
+        for g in range(PACK):
+            cols = slice(g * P, (g + 1) * P)
+            nc.scalar.copy(wo_bf[:, cols, :].rearrange("p (c i) j -> p c j i", i=4),
+                           wo_raw[:, :, cols].rearrange("p j (c i) -> p c j i", i=4))
+        wo_codes = keep.tile([P, F], U32, name="wo_codes", align_bytes=64)
+        wo_scales = keep.tile([P, F], U8, name="wo_scales", align_bytes=64)
+
+        x_rows = keep.tile([P, PACK, T], BF16, name="x_rows", align_bytes=64)
+        for j in range(PACK):
+            nc.vector.tensor_copy(page[j][:].indirect(offs2_sb[:]), v_sb[j][:])
+            if j >= 1:
+                nc.vector.tensor_tensor(x_rows[:, j - 1, :], page[j - 1][:], base_sb[:, j - 1, :], ADD)
+        nc.vector.quantize_mx(out=wo_codes[:].bitcast(FP8X4), scales=wo_scales[:],
+                              in_=wo_bf[:].rearrange("p f j -> p (f j)"))
+
+        last = PACK - 1
+        x_bf = [keep.tile([P, TC, PACK], BF16, name="x_bf%d" % c, align_bytes=64) for c in range(CHUNKS)]
+        x_codes = [keep.tile([P, TC], U32, name="x_codes%d" % c, align_bytes=64) for c in range(CHUNKS)]
+        x_scales = [keep.tile([P, TC], U8, name="x_scales%d" % c, align_bytes=64) for c in range(CHUNKS)]
+        y_sb = [keep.tile([P, PACK, TC], F32, name="y_sb%d" % c, align_bytes=64) for c in range(CHUNKS)]
+        out_rows = out.rearrange("(g p) t -> p g t", p=P)
+
+        def add_last(c):
+            ts = slice(c * TC, (c + 1) * TC)
+            nc.vector.tensor_tensor(x_rows[:, last, ts], page[last][:, ts], base_sb[:, last, ts], ADD)
+
+        def weave(c):
+            ts = slice(c * TC, (c + 1) * TC)
+            nc.vector.tensor_copy(x_bf[c][:].rearrange("p (c i) j -> p c j i", i=4),
+                                  x_rows[:, :, ts].rearrange("p j (c i) -> p c j i", i=4))
+
+        def finish(c):
+            ts = slice(c * TC, (c + 1) * TC)
+            nc.vector.quantize_mx(out=x_codes[c][:].bitcast(FP8X4), scales=x_scales[c][:],
+                                  in_=x_bf[c][:].rearrange("p t j -> p (t j)"))
+            y_ps = psum.tile([P, PACK, TC], F32, name="y_ps%d" % c)
+            for g in range(PACK):
+                cols = slice(g * P, (g + 1) * P)
+                nc.tensor.matmul_mx(out=y_ps[:, g, :], lhsT=wo_codes[:, cols].bitcast(FP8X4), lhsT_scale=wo_scales[:, cols],
+                                    rhs=x_codes[c][:].bitcast(FP8X4), rhs_scale=x_scales[c][:], start=True, stop=True)
+            nc.scalar.copy(y_sb[c][:], y_ps[:])
+            nc.sync.dma_start(out_rows[:, :, ts], y_sb[c][:])
+
+        for step in range(CHUNKS + 2):
+            if step < CHUNKS:
+                add_last(step)
+            if 0 <= step - 1 < CHUNKS:
+                weave(step - 1)
+            if 0 <= step - 2 < CHUNKS:
+                finish(step - 2)

@@ -19,7 +19,7 @@ P = 128
 PACK = 4
 HALVES = 2
 M_HALF = P // HALVES
-M_VECTOR = 40
+M_VECTOR = (16, 40)
 CHUNKS = 4
 TC = T // CHUNKS
 
@@ -40,16 +40,16 @@ def tile_attend_headpage_proj_kernel(tc, emb_words, emb_scales, wv, base, wo, of
         page = [keep.tile([P, T], F32, name="page%d" % j, align_bytes=64) for j in range(PACK)]
 
         nc.vector.memset(scales[:].bitcast(I32), 0)
-        nc.sync.dma_start(offs_sb[:], offs)
         wv_rows = wv.rearrange("(p j) e -> p j e", j=PACK)
-        for h in range(HALVES):
-            nc.sync.dma_start(wv_raw[h][:], wv_rows[:, :, h * (E // HALVES) : (h + 1) * (E // HALVES)])
-        nc.sync.dma_start(words[:].bitcast(I32), emb_words[0].bitcast(I32))
+        nc.sync.dma_start(wv_raw[0][:], wv_rows[:, :, : E // HALVES])
         for q in range(4):
-            nc.scalar.dma_start(scales[32 * q : 32 * q + 4, :].bitcast(I32), emb_scales[0, 4 * q : 4 * q + 4, :].bitcast(I32))
+            nc.sync.dma_start(scales[32 * q : 32 * q + 4, :].bitcast(I32), emb_scales[0, 4 * q : 4 * q + 4, :].bitcast(I32))
+        nc.sync.dma_start(offs_sb[:], offs)
+        nc.sync.dma_start(wv_raw[1][:], wv_rows[:, :, E // HALVES :])
+        nc.sync.dma_start(words[:].bitcast(I32), emb_words[0].bitcast(I32))
         nc.sync.dma_start(offs2_sb[:], offs2)
-        nc.sync.dma_start(base_sb[:], base.rearrange("(p j) t -> p j t", j=PACK))
         nc.sync.dma_start(wo_raw[:], wo.rearrange("(p j) f -> p j f", j=PACK))
+        nc.sync.dma_start(base_sb[:], base.rearrange("(p j) t -> p j t", j=PACK))
         for j in range(PACK):
             nc.vector.memset(page[j][:], 0.0)
 
@@ -60,17 +60,18 @@ def tile_attend_headpage_proj_kernel(tc, emb_words, emb_scales, wv, base, wo, of
         for h in range(HALVES):
             src = wv_raw[h][:].rearrange("p j (m t) -> p m t j", t=PACK)
             dst = wv_bf[:, :, h * M_HALF : (h + 1) * M_HALF, :].rearrange("p t m j -> p m t j")
-            nc.scalar.copy(dst[:, M_VECTOR:], src[:, M_VECTOR:])
-            nc.vector.tensor_copy(dst[:, :M_VECTOR], src[:, :M_VECTOR])
+            nc.scalar.copy(dst[:, M_VECTOR[h] :], src[:, M_VECTOR[h] :])
+            nc.vector.tensor_copy(dst[:, : M_VECTOR[h]], src[:, : M_VECTOR[h]])
         wv_codes = keep.tile([P, E], U32, name="wv_codes", align_bytes=64)
         wv_scales = keep.tile([P, E], U8, name="wv_scales", align_bytes=64)
+        got_words = keep.tile([P, I], U16, name="got_words", align_bytes=64)
         for j in range(PACK):
             cols = slice(j * P, (j + 1) * P)
+            if j == 1:
+                nc.vector.tensor_copy(got_words[:], words[:].indirect(offs_sb[:]))
             nc.vector.quantize_mx(out=wv_codes[:, cols].bitcast(FP8X4), scales=wv_scales[:, cols],
                                   in_=wv_bf[:, j].rearrange("p m j -> p (m j)"))
 
-        got_words = keep.tile([P, I], U16, name="got_words", align_bytes=64)
-        nc.vector.tensor_copy(got_words[:], words[:].indirect(offs_sb[:]))
 
         v_sb = [keep.tile([P, I], F32, name="v_sb%d" % j, align_bytes=64) for j in range(PACK)]
         for j in range(PACK):
@@ -80,7 +81,7 @@ def tile_attend_headpage_proj_kernel(tc, emb_words, emb_scales, wv, base, wo, of
                                 rhs=got_words[:].bitcast(FP4X4), rhs_scale=got_scales[:], start=True, stop=True)
             nc.scalar.copy(v_sb[j][:], v_ps[:])
 
-        wo_bf = keep.tile([P, F, PACK], BF16, name="wo_bf", align_bytes=64)
+        wo_bf = keep.tile([P, F, PACK], BF16, name="wo_bf", tag="woven", align_bytes=64)
         for g in range(PACK):
             cols = slice(g * P, (g + 1) * P)
             nc.scalar.copy(wo_bf[:, cols, :].rearrange("p (c i) j -> p c j i", i=4),
@@ -91,16 +92,15 @@ def tile_attend_headpage_proj_kernel(tc, emb_words, emb_scales, wv, base, wo, of
         x_rows = keep.tile([P, PACK, T], BF16, name="x_rows", align_bytes=64)
         for j in range(PACK):
             nc.vector.tensor_copy(page[j][:].indirect(offs2_sb[:]), v_sb[j][:])
-            if j >= 1:
-                nc.vector.tensor_tensor(x_rows[:, j - 1, :], page[j - 1][:], base_sb[:, j - 1, :], ADD)
+            if j < PACK - 1:
+                nc.gpsimd.tensor_tensor(x_rows[:, j, :], page[j][:], base_sb[:, j, :], ADD)
         nc.vector.quantize_mx(out=wo_codes[:].bitcast(FP8X4), scales=wo_scales[:],
                               in_=wo_bf[:].rearrange("p f j -> p (f j)"))
 
         last = PACK - 1
-        x_bf = [keep.tile([P, TC, PACK], BF16, name="x_bf%d" % c, align_bytes=64) for c in range(CHUNKS)]
+        x_bf = [keep.tile([P, TC, PACK], BF16, name="x_bf%d" % c, tag="woven" if c == 0 else "x_bf%d" % c, align_bytes=64) for c in range(CHUNKS)]
         x_codes = [keep.tile([P, TC], U32, name="x_codes%d" % c, align_bytes=64) for c in range(CHUNKS)]
         x_scales = [keep.tile([P, TC], U8, name="x_scales%d" % c, align_bytes=64) for c in range(CHUNKS)]
-        y_sb = [keep.tile([P, PACK, TC], F32, name="y_sb%d" % c, align_bytes=64) for c in range(CHUNKS)]
         out_rows = out.rearrange("(g p) t -> p g t", p=P)
 
         def add_last(c):
@@ -109,20 +109,28 @@ def tile_attend_headpage_proj_kernel(tc, emb_words, emb_scales, wv, base, wo, of
 
         def weave(c):
             ts = slice(c * TC, (c + 1) * TC)
-            nc.vector.tensor_copy(x_bf[c][:].rearrange("p (c i) j -> p c j i", i=4),
-                                  x_rows[:, :, ts].rearrange("p j (c i) -> p c j i", i=4))
+            copy = nc.scalar.copy if c == 1 else nc.vector.tensor_copy
+            copy(x_bf[c][:].rearrange("p (c i) j -> p c j i", i=4), x_rows[:, :, ts].rearrange("p j (c i) -> p c j i", i=4))
 
         def finish(c):
             ts = slice(c * TC, (c + 1) * TC)
             nc.vector.quantize_mx(out=x_codes[c][:].bitcast(FP8X4), scales=x_scales[c][:],
                                   in_=x_bf[c][:].rearrange("p t j -> p (t j)"))
-            y_ps = psum.tile([P, PACK, TC], F32, name="y_ps%d" % c)
-            for g in range(PACK):
-                cols = slice(g * P, (g + 1) * P)
-                nc.tensor.matmul_mx(out=y_ps[:, g, :], lhsT=wo_codes[:, cols].bitcast(FP8X4), lhsT_scale=wo_scales[:, cols],
-                                    rhs=x_codes[c][:].bitcast(FP8X4), rhs_scale=x_scales[c][:], start=True, stop=True)
-            nc.scalar.copy(y_sb[c][:], y_ps[:])
-            nc.sync.dma_start(out_rows[:, :, ts], y_sb[c][:])
+            parts = 2 if c == CHUNKS - 1 else 1
+            groups = PACK // parts
+            for part in range(parts):
+                y_ps = psum.tile([P, groups, TC], F32, name="y_ps%d_%d" % (c, part), tag="v_ps0" if part else "y_ps%d" % c)
+                gs = slice(part * groups, (part + 1) * groups)
+                for g in range(groups):
+                    cols = slice((part * groups + g) * P, (part * groups + g + 1) * P)
+                    nc.tensor.matmul_mx(out=y_ps[:, g, :], lhsT=wo_codes[:, cols].bitcast(FP8X4), lhsT_scale=wo_scales[:, cols],
+                                        rhs=x_codes[c][:].bitcast(FP8X4), rhs_scale=x_scales[c][:], start=True, stop=True)
+                y_sb = keep.tile([P, groups, TC], F32, name="y_sb%d_%d" % (c, part), align_bytes=64)
+                if part:
+                    nc.vector.tensor_copy(y_sb[:], y_ps[:])
+                else:
+                    nc.scalar.copy(y_sb[:], y_ps[:])
+                nc.sync.dma_start(out_rows[:, gs, ts], y_sb[:])
 
         for step in range(CHUNKS + 2):
             if step < CHUNKS:

@@ -1,6 +1,7 @@
 from contextlib import ExitStack
 
 import concourse.mybir as mybir
+from concourse.masks import make_identity
 
 K, U, I, T, E, F = 512, 2048, 256, 512, 512, 512
 FLOPS = 2 * K * E * I + 2 * E * F * T
@@ -19,9 +20,10 @@ P = 128
 PACK = 4
 HALVES = 2
 M_HALF = P // HALVES
-M_VECTOR = (16, 40)
+M_VECTOR = (16, 36)
 CHUNKS = 4
 TC = T // CHUNKS
+TURNED = 2
 
 
 def tile_attend_headpage_proj_kernel(tc, emb_words, emb_scales, wv, base, wo, offs, offs2, out):
@@ -32,52 +34,58 @@ def tile_attend_headpage_proj_kernel(tc, emb_words, emb_scales, wv, base, wo, of
 
         offs_sb = keep.tile([P, I // 16], U16, name="offs_sb")
         offs2_sb = keep.tile([P, I // 16], U16, name="offs2_sb")
-        words = keep.tile([P, U], U16, name="words", align_bytes=64)
+        words = keep.tile([P, U], U16, name="words", tag="words", align_bytes=64)
         scales = keep.tile([P, U], U8, name="scales", align_bytes=64)
         wv_raw = [keep.tile([P, PACK, E // HALVES], F32, name="wv_raw%d" % h, align_bytes=64) for h in range(HALVES)]
-        base_sb = keep.tile([P, PACK, T], F32, name="base_sb", align_bytes=64)
+        base_sb = [keep.tile([P, 2, T], F32, name="base_sb%d" % h, align_bytes=64) for h in range(2)]
         wo_raw = keep.tile([P, PACK, F], F32, name="wo_raw", align_bytes=64)
         page = [keep.tile([P, T], F32, name="page%d" % j, align_bytes=64) for j in range(PACK)]
+        ident_f32 = keep.tile([P, P], F32, name="ident_f32", align_bytes=64)
+        ident_bf = keep.tile([P, P], BF16, name="ident_bf", align_bytes=64)
+        make_identity(nc, ident_f32[:])
+        make_identity(nc, ident_bf[:])
 
         nc.vector.memset(scales[:].bitcast(I32), 0)
         wv_rows = wv.rearrange("(p j) e -> p j e", j=PACK)
         nc.sync.dma_start(wv_raw[0][:], wv_rows[:, :, : E // HALVES])
-        for q in range(4):
-            nc.sync.dma_start(scales[32 * q : 32 * q + 4, :].bitcast(I32), emb_scales[0, 4 * q : 4 * q + 4, :].bitcast(I32))
         nc.sync.dma_start(offs_sb[:], offs)
+        for r in range(4):
+            nc.sync.dma_start(scales[r:P:32, :].bitcast(I32), emb_scales[0, r:16:4, :].bitcast(I32))
         nc.sync.dma_start(wv_raw[1][:], wv_rows[:, :, E // HALVES :])
         nc.sync.dma_start(words[:].bitcast(I32), emb_words[0].bitcast(I32))
         nc.sync.dma_start(offs2_sb[:], offs2)
         nc.sync.dma_start(wo_raw[:], wo.rearrange("(p j) f -> p j f", j=PACK))
-        nc.sync.dma_start(base_sb[:], base.rearrange("(p j) t -> p j t", j=PACK))
+        base_rows = base.rearrange("(p j) t -> p j t", j=PACK)
+        nc.sync.dma_start(base_sb[0][:], base_rows[:, 0:2, :])
+        nc.sync.dma_start(base_sb[1][:], base_rows[:, 2:4, :])
         for j in range(PACK):
             nc.vector.memset(page[j][:], 0.0)
 
-        got_scales = keep.tile([P, I], U8, name="got_scales", align_bytes=64)
-        nc.vector.tensor_copy(got_scales[:], scales[:].indirect(offs_sb[:]))
-
         wv_bf = keep.tile([P, PACK, P, PACK], BF16, name="wv_bf", align_bytes=64)
+        got_scales = keep.tile([P, I], U8, name="got_scales", align_bytes=64)
         for h in range(HALVES):
             src = wv_raw[h][:].rearrange("p j (m t) -> p m t j", t=PACK)
             dst = wv_bf[:, :, h * M_HALF : (h + 1) * M_HALF, :].rearrange("p t m j -> p m t j")
             nc.scalar.copy(dst[:, M_VECTOR[h] :], src[:, M_VECTOR[h] :])
             nc.vector.tensor_copy(dst[:, : M_VECTOR[h]], src[:, : M_VECTOR[h]])
+            if h == 0:
+                nc.vector.tensor_copy(got_scales[:], scales[:].indirect(offs_sb[:]))
         wv_codes = keep.tile([P, E], U32, name="wv_codes", align_bytes=64)
-        wv_scales = keep.tile([P, E], U8, name="wv_scales", align_bytes=64)
+        first_scales = keep.tile([P, P], U8, name="first_scales", align_bytes=64)
         got_words = keep.tile([P, I], U16, name="got_words", align_bytes=64)
-        for j in range(PACK):
-            cols = slice(j * P, (j + 1) * P)
-            if j == 1:
-                nc.vector.tensor_copy(got_words[:], words[:].indirect(offs_sb[:]))
-            nc.vector.quantize_mx(out=wv_codes[:, cols].bitcast(FP8X4), scales=wv_scales[:, cols],
+        nc.vector.quantize_mx(out=wv_codes[:, :P].bitcast(FP8X4), scales=first_scales[:],
+                              in_=wv_bf[:, 0].rearrange("p m j -> p (m j)"))
+        nc.vector.tensor_copy(got_words[:], words[:].indirect(offs_sb[:]))
+        later_scales = keep.tile([P, E - P], U8, name="later_scales", tag="words", align_bytes=64)
+        wv_scales = [first_scales[:]] + [later_scales[:, (j - 1) * P : j * P] for j in range(1, PACK)]
+        for j in range(1, PACK):
+            nc.vector.quantize_mx(out=wv_codes[:, j * P : (j + 1) * P].bitcast(FP8X4), scales=wv_scales[j],
                                   in_=wv_bf[:, j].rearrange("p m j -> p (m j)"))
-
 
         v_sb = [keep.tile([P, I], F32, name="v_sb%d" % j, align_bytes=64) for j in range(PACK)]
         for j in range(PACK):
-            cols = slice(j * P, (j + 1) * P)
-            v_ps = psum.tile([P, I], F32, name="v_ps%d" % j)
-            nc.tensor.matmul_mx(out=v_ps[:], lhsT=wv_codes[:, cols].bitcast(FP8X4), lhsT_scale=wv_scales[:, cols],
+            v_ps = psum.tile([P, I], F32, name="v_ps%d" % j, tag="bank%d" % j)
+            nc.tensor.matmul_mx(out=v_ps[:], lhsT=wv_codes[:, j * P : (j + 1) * P].bitcast(FP8X4), lhsT_scale=wv_scales[j],
                                 rhs=got_words[:].bitcast(FP4X4), rhs_scale=got_scales[:], start=True, stop=True)
             nc.scalar.copy(v_sb[j][:], v_ps[:])
 
@@ -92,34 +100,48 @@ def tile_attend_headpage_proj_kernel(tc, emb_words, emb_scales, wv, base, wo, of
         x_rows = keep.tile([P, PACK, T], BF16, name="x_rows", align_bytes=64)
         for j in range(PACK):
             nc.vector.tensor_copy(page[j][:].indirect(offs2_sb[:]), v_sb[j][:])
-            if j < PACK - 1:
-                nc.gpsimd.tensor_tensor(x_rows[:, j, :], page[j][:], base_sb[:, j, :], ADD)
+            if j < TURNED:
+                turned_ps = psum.tile([P, T], F32, name="turned_ps%d" % j, tag="bank%d" % (4 + j))
+                for b in range(T // P):
+                    ts = slice(b * P, (b + 1) * P)
+                    nc.tensor.matmul(turned_ps[:, ts], lhsT=base_sb[j // 2][:, j % 2, ts], rhs=ident_f32[:], is_transpose=True, start=True, stop=False)
+                    nc.tensor.matmul(turned_ps[:, ts], lhsT=page[j][:, ts], rhs=ident_f32[:], is_transpose=True, start=False, stop=True)
+                turned = keep.tile([P, T], BF16, name="turned%d" % j, align_bytes=64)
+                nc.scalar.copy(turned[:], turned_ps[:])
+                back_ps = psum.tile([P, T], BF16, name="back_ps%d" % j, tag="bank%d" % j)
+                for b in range(T // P):
+                    ts = slice(b * P, (b + 1) * P)
+                    nc.tensor.transpose(back_ps[:, ts], turned[:, ts], ident_bf[:])
+                nc.scalar.copy(x_rows[:, j, :], back_ps[:])
+            elif j < PACK - 1:
+                nc.vector.tensor_tensor(x_rows[:, j, :], page[j][:], base_sb[1][:, j - 2, :], ADD)
         nc.vector.quantize_mx(out=wo_codes[:].bitcast(FP8X4), scales=wo_scales[:],
                               in_=wo_bf[:].rearrange("p f j -> p (f j)"))
 
         last = PACK - 1
-        x_bf = [keep.tile([P, TC, PACK], BF16, name="x_bf%d" % c, tag="woven" if c == 0 else "x_bf%d" % c, align_bytes=64) for c in range(CHUNKS)]
+        x_bf = [keep.tile([P, TC, PACK], BF16, name="x_bf%d" % c, tag="woven" if c == 0 else "x_bf%d" % c, align_bytes=64)
+                for c in range(CHUNKS)]
         x_codes = [keep.tile([P, TC], U32, name="x_codes%d" % c, align_bytes=64) for c in range(CHUNKS)]
         x_scales = [keep.tile([P, TC], U8, name="x_scales%d" % c, align_bytes=64) for c in range(CHUNKS)]
         out_rows = out.rearrange("(g p) t -> p g t", p=P)
 
         def add_last(c):
             ts = slice(c * TC, (c + 1) * TC)
-            nc.vector.tensor_tensor(x_rows[:, last, ts], page[last][:, ts], base_sb[:, last, ts], ADD)
+            nc.vector.tensor_tensor(x_rows[:, last, ts], page[last][:, ts], base_sb[1][:, last - 2, ts], ADD)
 
         def weave(c):
             ts = slice(c * TC, (c + 1) * TC)
-            copy = nc.scalar.copy if c == 1 else nc.vector.tensor_copy
+            copy = nc.scalar.copy if c in (1,) else nc.vector.tensor_copy
             copy(x_bf[c][:].rearrange("p (c i) j -> p c j i", i=4), x_rows[:, :, ts].rearrange("p j (c i) -> p c j i", i=4))
 
         def finish(c):
             ts = slice(c * TC, (c + 1) * TC)
             nc.vector.quantize_mx(out=x_codes[c][:].bitcast(FP8X4), scales=x_scales[c][:],
                                   in_=x_bf[c][:].rearrange("p t j -> p (t j)"))
-            parts = 2 if c == CHUNKS - 1 else 1
+            parts = 2 if c >= CHUNKS - 2 else 1
             groups = PACK // parts
             for part in range(parts):
-                y_ps = psum.tile([P, groups, TC], F32, name="y_ps%d_%d" % (c, part), tag="v_ps0" if part else "y_ps%d" % c)
+                y_ps = psum.tile([P, groups, TC], F32, name="y_ps%d_%d" % (c, part), tag="bank%d" % ((6, 7, 2, 4)[c] + part))
                 gs = slice(part * groups, (part + 1) * groups)
                 for g in range(groups):
                     cols = slice((part * groups + g) * P, (part * groups + g + 1) * P)

@@ -23,7 +23,7 @@ M_HALF = P // HALVES
 M_VECTOR = (16, 36)
 CHUNKS = 4
 TC = T // CHUNKS
-TURNED = 2
+TURNED = 3
 
 
 def tile_attend_headpage_proj_kernel(tc, emb_words, emb_scales, wv, base, wo, offs, offs2, out):
@@ -82,12 +82,19 @@ def tile_attend_headpage_proj_kernel(tc, emb_words, emb_scales, wv, base, wo, of
             nc.vector.quantize_mx(out=wv_codes[:, j * P : (j + 1) * P].bitcast(FP8X4), scales=wv_scales[j],
                                   in_=wv_bf[:, j].rearrange("p m j -> p (m j)"))
 
-        v_sb = [keep.tile([P, I], F32, name="v_sb%d" % j, align_bytes=64) for j in range(PACK)]
-        for j in range(PACK):
-            v_ps = psum.tile([P, I], F32, name="v_ps%d" % j, tag="bank%d" % j)
-            nc.tensor.matmul_mx(out=v_ps[:], lhsT=wv_codes[:, j * P : (j + 1) * P].bitcast(FP8X4), lhsT_scale=wv_scales[j],
+        def project(j, v_ps):
+            nc.tensor.matmul_mx(out=v_ps, lhsT=wv_codes[:, j * P : (j + 1) * P].bitcast(FP8X4), lhsT_scale=wv_scales[j],
                                 rhs=got_words[:].bitcast(FP4X4), rhs_scale=got_scales[:], start=True, stop=True)
-            nc.scalar.copy(v_sb[j][:], v_ps[:])
+
+        v_sb = keep.tile([P, PACK * I], F32, name="v_sb", align_bytes=64)
+        for j in range(2):
+            v_ps = psum.tile([P, I], F32, name="v_ps%d" % j, tag="bank%d" % j)
+            project(j, v_ps[:])
+            nc.vector.tensor_copy(v_sb[:, j * I : (j + 1) * I], v_ps[:])
+        v_ps = psum.tile([P, 2 * I], F32, name="v_ps2", tag="bank2")
+        for j in range(2, PACK):
+            project(j, v_ps[:, (j - 2) * I : (j - 1) * I])
+        nc.scalar.copy(v_sb[:, 2 * I :], v_ps[:])
 
         wo_bf = keep.tile([P, F, PACK], BF16, name="wo_bf", tag="woven", align_bytes=64)
         for g in range(PACK):
@@ -99,34 +106,39 @@ def tile_attend_headpage_proj_kernel(tc, emb_words, emb_scales, wv, base, wo, of
 
         x_rows = keep.tile([P, PACK, T], BF16, name="x_rows", align_bytes=64)
         for j in range(PACK):
-            nc.vector.tensor_copy(page[j][:].indirect(offs2_sb[:]), v_sb[j][:])
+            nc.vector.tensor_copy(page[j][:].indirect(offs2_sb[:]), v_sb[:, j * I : (j + 1) * I])
             if j < TURNED:
-                turned_ps = psum.tile([P, T], F32, name="turned_ps%d" % j, tag="bank%d" % (4 + j))
+                turned_ps = psum.tile([P, T], F32, name="turned_ps%d" % j, tag="bank%d" % (4 + j % 2))
                 for b in range(T // P):
                     ts = slice(b * P, (b + 1) * P)
-                    nc.tensor.matmul(turned_ps[:, ts], lhsT=base_sb[j // 2][:, j % 2, ts], rhs=ident_f32[:], is_transpose=True, start=True, stop=False)
-                    nc.tensor.matmul(turned_ps[:, ts], lhsT=page[j][:, ts], rhs=ident_f32[:], is_transpose=True, start=False, stop=True)
-                turned = keep.tile([P, T], BF16, name="turned%d" % j, align_bytes=64)
+                    nc.tensor.matmul(turned_ps[:, ts], lhsT=base_sb[j // 2][:, j % 2, ts], rhs=ident_f32[:],
+                                     is_transpose=True, start=(b == 0), stop=False)
+                for b in range(T // P):
+                    ts = slice(b * P, (b + 1) * P)
+                    nc.tensor.matmul(turned_ps[:, ts], lhsT=page[j][:, ts], rhs=ident_f32[:],
+                                     is_transpose=True, start=False, stop=(b == T // P - 1))
+                turned = keep.tile([P, T], BF16, name="turned%d" % j, tag="turned%d" % j, align_bytes=64)
                 nc.scalar.copy(turned[:], turned_ps[:])
-                back_ps = psum.tile([P, T], BF16, name="back_ps%d" % j, tag="bank%d" % j)
-                for b in range(T // P):
-                    ts = slice(b * P, (b + 1) * P)
-                    nc.tensor.transpose(back_ps[:, ts], turned[:, ts], ident_bf[:])
-                nc.scalar.copy(x_rows[:, j, :], back_ps[:])
-            elif j < PACK - 1:
-                nc.vector.tensor_tensor(x_rows[:, j, :], page[j][:], base_sb[1][:, j - 2, :], ADD)
+                parts = 2 if j == TURNED - 1 else 1
+                width = T // parts
+                for part in range(parts):
+                    back_ps = psum.tile([P, width], BF16, name="back_ps%d_%d" % (j, part), tag="bank%d" % (j + part))
+                    for b in range(width // P):
+                        ts = slice(part * width + b * P, part * width + (b + 1) * P)
+                        nc.tensor.transpose(back_ps[:, b * P : (b + 1) * P], turned[:, ts], ident_bf[:])
+                    nc.scalar.copy(x_rows[:, j, part * width : (part + 1) * width], back_ps[:])
         nc.vector.quantize_mx(out=wo_codes[:].bitcast(FP8X4), scales=wo_scales[:],
                               in_=wo_bf[:].rearrange("p f j -> p (f j)"))
 
         last = PACK - 1
-        x_bf = [keep.tile([P, TC, PACK], BF16, name="x_bf%d" % c, tag="woven" if c == 0 else "x_bf%d" % c, align_bytes=64)
+        x_bf = [keep.tile([P, TC, PACK], BF16, name="x_bf%d" % c, tag=("woven", "turned2", "x_bf2", "x_bf3")[c], align_bytes=64)
                 for c in range(CHUNKS)]
         x_codes = [keep.tile([P, TC], U32, name="x_codes%d" % c, align_bytes=64) for c in range(CHUNKS)]
         x_scales = [keep.tile([P, TC], U8, name="x_scales%d" % c, align_bytes=64) for c in range(CHUNKS)]
         out_rows = out.rearrange("(g p) t -> p g t", p=P)
 
-        def add_last(c):
-            ts = slice(c * TC, (c + 1) * TC)
+        def add_last(h):
+            ts = slice(h * T // 2, (h + 1) * T // 2)
             nc.vector.tensor_tensor(x_rows[:, last, ts], page[last][:, ts], base_sb[1][:, last - 2, ts], ADD)
 
         def weave(c):
@@ -141,7 +153,7 @@ def tile_attend_headpage_proj_kernel(tc, emb_words, emb_scales, wv, base, wo, of
             parts = 2 if c >= CHUNKS - 2 else 1
             groups = PACK // parts
             for part in range(parts):
-                y_ps = psum.tile([P, groups, TC], F32, name="y_ps%d_%d" % (c, part), tag="bank%d" % ((6, 7, 2, 4)[c] + part))
+                y_ps = psum.tile([P, groups, TC], F32, name="y_ps%d_%d" % (c, part), tag="bank%d" % ((6, 7, 0, 4)[c] + part))
                 gs = slice(part * groups, (part + 1) * groups)
                 for g in range(groups):
                     cols = slice((part * groups + g) * P, (part * groups + g + 1) * P)
@@ -154,10 +166,10 @@ def tile_attend_headpage_proj_kernel(tc, emb_words, emb_scales, wv, base, wo, of
                     nc.scalar.copy(y_sb[:], y_ps[:])
                 nc.sync.dma_start(out_rows[:, gs, ts], y_sb[:])
 
-        for step in range(CHUNKS + 2):
+        for h in range(2):
+            add_last(h)
+        for step in range(CHUNKS + 1):
             if step < CHUNKS:
-                add_last(step)
-            if 0 <= step - 1 < CHUNKS:
-                weave(step - 1)
-            if 0 <= step - 2 < CHUNKS:
-                finish(step - 2)
+                weave(step)
+            if step >= 1:
+                finish(step - 1)

@@ -18,12 +18,17 @@ ADD = mybir.AluOpType.add
 
 P = 128
 PACK = 4
-HALVES = 2
-M_HALF = P // HALVES
+LIST_ROWS = 16
+QUADRANT = 32
+SCALE_ROWS = K // 32
+M_HALF = P // 2
 M_VECTOR = (16, 36)
+T_HALF = T // 2
 CHUNKS = 4
-TC = T // CHUNKS
-TURNED = 3
+T_CHUNK = T // CHUNKS
+SCALAR_WEAVES = 2
+SHARED_COPIES = 2
+LAST = PACK - 1
 
 
 def tile_attend_headpage_proj_kernel(tc, emb_words, emb_scales, wv, base, wo, offs, offs2, out):
@@ -32,11 +37,11 @@ def tile_attend_headpage_proj_kernel(tc, emb_words, emb_scales, wv, base, wo, of
         keep = ctx.enter_context(tc.tile_pool(name="keep", bufs=1))
         psum = ctx.enter_context(tc.psum_pool(name="psum", bufs=1))
 
-        offs_sb = keep.tile([P, I // 16], U16, name="offs_sb")
-        offs2_sb = keep.tile([P, I // 16], U16, name="offs2_sb")
+        offs_sb = keep.tile([P, I // LIST_ROWS], U16, name="offs_sb")
+        offs2_sb = keep.tile([P, I // LIST_ROWS], U16, name="offs2_sb")
         words = keep.tile([P, U], U16, name="words", tag="words", align_bytes=64)
         scales = keep.tile([P, U], U8, name="scales", align_bytes=64)
-        wv_raw = [keep.tile([P, PACK, E // HALVES], F32, name="wv_raw%d" % h, align_bytes=64) for h in range(HALVES)]
+        wv_raw = [keep.tile([P, PACK, E // 2], F32, name="wv_raw%d" % h, align_bytes=64) for h in range(2)]
         base_sb = [keep.tile([P, 2, T], F32, name="base_sb%d" % h, align_bytes=64) for h in range(2)]
         wo_raw = keep.tile([P, PACK, F], F32, name="wo_raw", align_bytes=64)
         page = [keep.tile([P, T], F32, name="page%d" % j, align_bytes=64) for j in range(PACK)]
@@ -47,11 +52,11 @@ def tile_attend_headpage_proj_kernel(tc, emb_words, emb_scales, wv, base, wo, of
 
         nc.vector.memset(scales[:].bitcast(I32), 0)
         wv_rows = wv.rearrange("(p j) e -> p j e", j=PACK)
-        nc.sync.dma_start(wv_raw[0][:], wv_rows[:, :, : E // HALVES])
+        nc.sync.dma_start(wv_raw[0][:], wv_rows[:, :, : E // 2])
         nc.sync.dma_start(offs_sb[:], offs)
         for r in range(4):
-            nc.sync.dma_start(scales[r:P:32, :].bitcast(I32), emb_scales[0, r:16:4, :].bitcast(I32))
-        nc.sync.dma_start(wv_raw[1][:], wv_rows[:, :, E // HALVES :])
+            nc.sync.dma_start(scales[r:P:QUADRANT, :].bitcast(I32), emb_scales[0, r:SCALE_ROWS:4, :].bitcast(I32))
+        nc.sync.dma_start(wv_raw[1][:], wv_rows[:, :, E // 2 :])
         nc.sync.dma_start(words[:].bitcast(I32), emb_words[0].bitcast(I32))
         nc.sync.dma_start(offs2_sb[:], offs2)
         nc.sync.dma_start(wo_raw[:], wo.rearrange("(p j) f -> p j f", j=PACK))
@@ -61,26 +66,30 @@ def tile_attend_headpage_proj_kernel(tc, emb_words, emb_scales, wv, base, wo, of
         for j in range(PACK):
             nc.vector.memset(page[j][:], 0.0)
 
+        def base_row(j):
+            return base_sb[j // 2][:, j % 2, :]
+
         wv_bf = keep.tile([P, PACK, P, PACK], BF16, name="wv_bf", align_bytes=64)
         got_scales = keep.tile([P, I], U8, name="got_scales", align_bytes=64)
-        for h in range(HALVES):
-            src = wv_raw[h][:].rearrange("p j (m t) -> p m t j", t=PACK)
-            dst = wv_bf[:, :, h * M_HALF : (h + 1) * M_HALF, :].rearrange("p t m j -> p m t j")
+        for h in range(2):
+            src = wv_raw[h][:].rearrange("p r (m j) -> p m j r", j=PACK)
+            dst = wv_bf[:, :, h * M_HALF : (h + 1) * M_HALF, :].rearrange("p j m r -> p m j r")
             nc.scalar.copy(dst[:, M_VECTOR[h] :], src[:, M_VECTOR[h] :])
             nc.vector.tensor_copy(dst[:, : M_VECTOR[h]], src[:, : M_VECTOR[h]])
             if h == 0:
                 nc.vector.tensor_copy(got_scales[:], scales[:].indirect(offs_sb[:]))
+
         wv_codes = keep.tile([P, E], U32, name="wv_codes", align_bytes=64)
         first_scales = keep.tile([P, P], U8, name="first_scales", align_bytes=64)
         got_words = keep.tile([P, I], U16, name="got_words", align_bytes=64)
         nc.vector.quantize_mx(out=wv_codes[:, :P].bitcast(FP8X4), scales=first_scales[:],
-                              in_=wv_bf[:, 0].rearrange("p m j -> p (m j)"))
+                              in_=wv_bf[:, 0].rearrange("p m r -> p (m r)"))
         nc.vector.tensor_copy(got_words[:], words[:].indirect(offs_sb[:]))
         later_scales = keep.tile([P, E - P], U8, name="later_scales", tag="words", align_bytes=64)
         wv_scales = [first_scales[:]] + [later_scales[:, (j - 1) * P : j * P] for j in range(1, PACK)]
         for j in range(1, PACK):
             nc.vector.quantize_mx(out=wv_codes[:, j * P : (j + 1) * P].bitcast(FP8X4), scales=wv_scales[j],
-                                  in_=wv_bf[:, j].rearrange("p m j -> p (m j)"))
+                                  in_=wv_bf[:, j].rearrange("p m r -> p (m r)"))
 
         def project(j, v_ps):
             nc.tensor.matmul_mx(out=v_ps, lhsT=wv_codes[:, j * P : (j + 1) * P].bitcast(FP8X4), lhsT_scale=wv_scales[j],
@@ -96,80 +105,90 @@ def tile_attend_headpage_proj_kernel(tc, emb_words, emb_scales, wv, base, wo, of
             project(j, v_ps[:, (j - 2) * I : (j - 1) * I])
         nc.scalar.copy(v_sb[:, 2 * I :], v_ps[:])
 
-        wo_bf = keep.tile([P, F, PACK], BF16, name="wo_bf", tag="woven", align_bytes=64)
-        for g in range(PACK):
-            cols = slice(g * P, (g + 1) * P)
-            nc.scalar.copy(wo_bf[:, cols, :].rearrange("p (c i) j -> p c j i", i=4),
-                           wo_raw[:, :, cols].rearrange("p j (c i) -> p c j i", i=4))
+        wo_bf = [keep.tile([P, F // 2, PACK], BF16, name="wo_bf%d" % h, align_bytes=64) for h in range(2)]
+        for g in range(F // P):
+            nc.scalar.copy(wo_bf[g // 2][:, g % 2 * P : (g % 2 + 1) * P, :].rearrange("p (c i) j -> p c j i", i=4),
+                           wo_raw[:, :, g * P : (g + 1) * P].rearrange("p j (c i) -> p c j i", i=4))
         wo_codes = keep.tile([P, F], U32, name="wo_codes", align_bytes=64)
-        wo_scales = keep.tile([P, F], U8, name="wo_scales", align_bytes=64)
+        wo_scales = []
 
-        x_rows = keep.tile([P, PACK, T], BF16, name="x_rows", align_bytes=64)
+        def quantise_wo(h, tag):
+            wo_scales.append(keep.tile([P, F // 2], U8, name="wo_scales%d" % h, tag=tag, align_bytes=64))
+            nc.vector.quantize_mx(out=wo_codes[:, h * F // 2 : (h + 1) * F // 2].bitcast(FP8X4), scales=wo_scales[h][:],
+                                  in_=wo_bf[h][:].rearrange("p f j -> p (f j)"))
+
+        x_rows = keep.tile([P, 2, PACK, T_HALF], BF16, name="x_rows", align_bytes=64)
+
+        def add_by_transposes(j, first_place, parts):
+            width = T - first_place
+            blocks = [(slice(c, c + P), slice(first_place + c, first_place + c + P)) for c in range(0, width, P)]
+            turned_ps = psum.tile([P, width], F32, name="turned_ps%d" % j, tag="bank%d" % (4 + j % 2))
+            for b, (cols, places) in enumerate(blocks):
+                nc.tensor.matmul(turned_ps[:, cols], lhsT=base_row(j)[:, places], rhs=ident_f32[:],
+                                 is_transpose=True, start=(b == 0), stop=False)
+            for b, (cols, places) in enumerate(blocks):
+                nc.tensor.matmul(turned_ps[:, cols], lhsT=page[j][:, places], rhs=ident_f32[:],
+                                 is_transpose=True, start=False, stop=(b == len(blocks) - 1))
+            part_width = width // parts
+            turned = [keep.tile([P, part_width], BF16, name="turned%d_%d" % (j, part), tag="turned%d_%d" % (j, part), align_bytes=64)
+                      for part in range(parts)]
+            for part in range(parts):
+                nc.scalar.copy(turned[part][:], turned_ps[:, part * part_width : (part + 1) * part_width])
+            back_ps = psum.tile([P, width], BF16, name="back_ps%d" % j, tag="bank%d" % j)
+            for cols, places in blocks:
+                part, col = divmod(cols.start, part_width)
+                nc.tensor.transpose(back_ps[:, cols], turned[part][:, col : col + P], ident_bf[:])
+            nc.scalar.copy(x_rows[:, first_place // T_HALF :, j, :], back_ps[:].rearrange("p (h t) -> p h t", t=T_HALF))
+
         for j in range(PACK):
             nc.vector.tensor_copy(page[j][:].indirect(offs2_sb[:]), v_sb[:, j * I : (j + 1) * I])
-            if j < TURNED:
-                turned_ps = psum.tile([P, T], F32, name="turned_ps%d" % j, tag="bank%d" % (4 + j % 2))
-                for b in range(T // P):
-                    ts = slice(b * P, (b + 1) * P)
-                    nc.tensor.matmul(turned_ps[:, ts], lhsT=base_sb[j // 2][:, j % 2, ts], rhs=ident_f32[:],
-                                     is_transpose=True, start=(b == 0), stop=False)
-                for b in range(T // P):
-                    ts = slice(b * P, (b + 1) * P)
-                    nc.tensor.matmul(turned_ps[:, ts], lhsT=page[j][:, ts], rhs=ident_f32[:],
-                                     is_transpose=True, start=False, stop=(b == T // P - 1))
-                turned = keep.tile([P, T], BF16, name="turned%d" % j, tag="turned%d" % j, align_bytes=64)
-                nc.scalar.copy(turned[:], turned_ps[:])
-                parts = 2 if j == TURNED - 1 else 1
-                width = T // parts
-                for part in range(parts):
-                    back_ps = psum.tile([P, width], BF16, name="back_ps%d_%d" % (j, part), tag="bank%d" % (j + part))
-                    for b in range(width // P):
-                        ts = slice(part * width + b * P, part * width + (b + 1) * P)
-                        nc.tensor.transpose(back_ps[:, b * P : (b + 1) * P], turned[:, ts], ident_bf[:])
-                    nc.scalar.copy(x_rows[:, j, part * width : (part + 1) * width], back_ps[:])
-        nc.vector.quantize_mx(out=wo_codes[:].bitcast(FP8X4), scales=wo_scales[:],
-                              in_=wo_bf[:].rearrange("p f j -> p (f j)"))
+            if j < LAST - 1:
+                add_by_transposes(j, 0, 1)
+            elif j == LAST - 1:
+                add_by_transposes(j, T_HALF, SCALAR_WEAVES)
+        quantise_wo(0, "wo_scales0")
 
-        last = PACK - 1
-        x_bf = [keep.tile([P, TC, PACK], BF16, name="x_bf%d" % c, tag=("woven", "turned2", "x_bf2", "x_bf3")[c], align_bytes=64)
-                for c in range(CHUNKS)]
-        x_codes = [keep.tile([P, TC], U32, name="x_codes%d" % c, align_bytes=64) for c in range(CHUNKS)]
-        x_scales = [keep.tile([P, TC], U8, name="x_scales%d" % c, align_bytes=64) for c in range(CHUNKS)]
+        x_tags = ["turned%d_%d" % (LAST - 1, c) if c < SCALAR_WEAVES else "x_bf%d" % c for c in range(CHUNKS)]
+        x_bf = [keep.tile([P, T_CHUNK, PACK], BF16, name="x_bf%d" % c, tag=x_tags[c], align_bytes=64) for c in range(CHUNKS)]
+        x_codes = [keep.tile([P, T_CHUNK], U32, name="x_codes%d" % c, align_bytes=64) for c in range(CHUNKS)]
+        x_scales = [keep.tile([P, T_CHUNK], U8, name="x_scales%d" % c, align_bytes=64) for c in range(CHUNKS)]
         out_rows = out.rearrange("(g p) t -> p g t", p=P)
+        y_banks = (6, 0, 4, 2)
 
-        def add_last(h):
-            ts = slice(h * T // 2, (h + 1) * T // 2)
-            nc.vector.tensor_tensor(x_rows[:, last, ts], page[last][:, ts], base_sb[1][:, last - 2, ts], ADD)
+        def add_on_vector(j, h):
+            places = slice(h * T_HALF, (h + 1) * T_HALF)
+            nc.vector.tensor_tensor(x_rows[:, h, j, :], page[j][:, places], base_row(j)[:, places], ADD)
 
         def weave(c):
-            ts = slice(c * TC, (c + 1) * TC)
-            copy = nc.scalar.copy if c in (1,) else nc.vector.tensor_copy
-            copy(x_bf[c][:].rearrange("p (c i) j -> p c j i", i=4), x_rows[:, :, ts].rearrange("p j (c i) -> p c j i", i=4))
+            half, at = divmod(c * T_CHUNK, T_HALF)
+            copy = nc.scalar.copy if c < SCALAR_WEAVES else nc.vector.tensor_copy
+            copy(x_bf[c][:].rearrange("p (c i) j -> p c j i", i=4),
+                 x_rows[:, half, :, at : at + T_CHUNK].rearrange("p j (c i) -> p c j i", i=4))
 
-        def finish(c):
-            ts = slice(c * TC, (c + 1) * TC)
+        def multiply(c):
+            places = slice(c * T_CHUNK, (c + 1) * T_CHUNK)
             nc.vector.quantize_mx(out=x_codes[c][:].bitcast(FP8X4), scales=x_scales[c][:],
                                   in_=x_bf[c][:].rearrange("p t j -> p (t j)"))
-            parts = 2 if c >= CHUNKS - 2 else 1
-            groups = PACK // parts
-            for part in range(parts):
-                y_ps = psum.tile([P, groups, TC], F32, name="y_ps%d_%d" % (c, part), tag="bank%d" % ((6, 7, 0, 4)[c] + part))
-                gs = slice(part * groups, (part + 1) * groups)
-                for g in range(groups):
-                    cols = slice((part * groups + g) * P, (part * groups + g + 1) * P)
-                    nc.tensor.matmul_mx(out=y_ps[:, g, :], lhsT=wo_codes[:, cols].bitcast(FP8X4), lhsT_scale=wo_scales[:, cols],
+            if c == 0:
+                quantise_wo(1, x_tags[0])
+            for h in range(2):
+                y_ps = psum.tile([P, 2, T_CHUNK], F32, name="y_ps%d_%d" % (c, h), tag="bank%d" % (y_banks[c] + h))
+                for g in range(2):
+                    cols = slice((2 * h + g) * P, (2 * h + g + 1) * P)
+                    nc.tensor.matmul_mx(out=y_ps[:, g, :], lhsT=wo_codes[:, cols].bitcast(FP8X4), lhsT_scale=wo_scales[h][:, g * P : (g + 1) * P],
                                         rhs=x_codes[c][:].bitcast(FP8X4), rhs_scale=x_scales[c][:], start=True, stop=True)
-                y_sb = keep.tile([P, groups, TC], F32, name="y_sb%d_%d" % (c, part), align_bytes=64)
-                if part:
+                y_sb = keep.tile([P, 2, T_CHUNK], F32, name="y_sb%d_%d" % (c, h), align_bytes=64)
+                if h == 1 and c >= CHUNKS - SHARED_COPIES:
                     nc.vector.tensor_copy(y_sb[:], y_ps[:])
                 else:
                     nc.scalar.copy(y_sb[:], y_ps[:])
-                nc.sync.dma_start(out_rows[:, gs, ts], y_sb[:])
+                nc.sync.dma_start(out_rows[:, 2 * h : 2 * h + 2, places], y_sb[:])
 
-        for h in range(2):
-            add_last(h)
+        add_on_vector(LAST - 1, 0)
+        add_on_vector(LAST, 0)
+        add_on_vector(LAST, 1)
         for step in range(CHUNKS + 1):
             if step < CHUNKS:
                 weave(step)
             if step >= 1:
-                finish(step - 1)
+                multiply(step - 1)

@@ -23,12 +23,8 @@ QUADRANT = 32
 SCALE_ROWS = K // 32
 M_HALF = P // 2
 M_VECTOR = (16, 36)
-T_HALF = T // 2
-CHUNKS = 4
-T_CHUNK = T // CHUNKS
-SCALAR_WEAVES = 2
-SHARED_COPIES = 2
-LAST = PACK - 1
+CHUNKS = T // P
+BANK = 512
 
 
 def tile_attend_headpage_proj_kernel(tc, emb_words, emb_scales, wv, base, wo, offs, offs2, out):
@@ -37,21 +33,27 @@ def tile_attend_headpage_proj_kernel(tc, emb_words, emb_scales, wv, base, wo, of
         keep = ctx.enter_context(tc.tile_pool(name="keep", bufs=1))
         psum = ctx.enter_context(tc.psum_pool(name="psum", bufs=1))
 
+        def sbuf(shape, dtype, name, tag=None):
+            return keep.tile(shape, dtype, name=name, tag=tag or name, align_bytes=64)
+
+        def bank(shape, dtype, name, b):
+            return psum.tile(shape, dtype, name=name, tag="bank%d" % b)
+
         offs_sb = keep.tile([P, I // LIST_ROWS], U16, name="offs_sb")
         offs2_sb = keep.tile([P, I // LIST_ROWS], U16, name="offs2_sb")
-        words = keep.tile([P, U], U16, name="words", tag="words", align_bytes=64)
-        scales = keep.tile([P, U], U8, name="scales", align_bytes=64)
-        wv_raw = [keep.tile([P, PACK, E // 2], F32, name="wv_raw%d" % h, align_bytes=64) for h in range(2)]
-        base_sb = [keep.tile([P, 2, T], F32, name="base_sb%d" % h, align_bytes=64) for h in range(2)]
-        wo_raw = keep.tile([P, PACK, F], F32, name="wo_raw", align_bytes=64)
-        page = [keep.tile([P, T], F32, name="page%d" % j, align_bytes=64) for j in range(PACK)]
-        ident_f32 = keep.tile([P, P], F32, name="ident_f32", align_bytes=64)
-        ident_bf = keep.tile([P, P], BF16, name="ident_bf", align_bytes=64)
-        make_identity(nc, ident_f32[:])
-        make_identity(nc, ident_bf[:])
+        words = sbuf([P, U], U16, "words")
+        scales = sbuf([P, U], U8, "scales")
+        wv_raw = [sbuf([P, PACK, E // 2], F32, "wv_raw%d" % h) for h in range(2)]
+        base_sb = [sbuf([P, 2, T], F32, "base_sb%d" % u) for u in range(2)]
+        wo_raw = sbuf([P, PACK, F], F32, "wo_raw")
+        page = [sbuf([P, T], F32, "page%d" % j) for j in range(PACK)]
+        ident_f32 = sbuf([P, P], F32, "ident_f32")
+        ident_bf = sbuf([P, P], BF16, "ident_bf")
 
         nc.vector.memset(scales[:].bitcast(I32), 0)
-        wv_rows = wv.rearrange("(p j) e -> p j e", j=PACK)
+        make_identity(nc, ident_f32[:])
+        make_identity(nc, ident_bf[:])
+        wv_rows = wv.rearrange("(p r) e -> p r e", r=PACK)
         nc.sync.dma_start(wv_raw[0][:], wv_rows[:, :, : E // 2])
         nc.sync.dma_start(offs_sb[:], offs)
         for r in range(4):
@@ -61,16 +63,17 @@ def tile_attend_headpage_proj_kernel(tc, emb_words, emb_scales, wv, base, wo, of
         nc.sync.dma_start(offs2_sb[:], offs2)
         nc.sync.dma_start(wo_raw[:], wo.rearrange("(p j) f -> p j f", j=PACK))
         base_rows = base.rearrange("(p j) t -> p j t", j=PACK)
-        nc.sync.dma_start(base_sb[0][:], base_rows[:, 0:2, :])
-        nc.sync.dma_start(base_sb[1][:], base_rows[:, 2:4, :])
+        for u in range(2):
+            nc.sync.dma_start(base_sb[u][:], base_rows[:, 2 * u : 2 * u + 2, :])
         for j in range(PACK):
             nc.vector.memset(page[j][:], 0.0)
 
         def base_row(j):
             return base_sb[j // 2][:, j % 2, :]
 
-        wv_bf = keep.tile([P, PACK, P, PACK], BF16, name="wv_bf", align_bytes=64)
-        got_scales = keep.tile([P, I], U8, name="got_scales", align_bytes=64)
+        got_scales = sbuf([P, I], U8, "got_scales")
+
+        wv_bf = sbuf([P, PACK, P, PACK], BF16, "wv_bf")
         for h in range(2):
             src = wv_raw[h][:].rearrange("p r (m j) -> p m j r", j=PACK)
             dst = wv_bf[:, :, h * M_HALF : (h + 1) * M_HALF, :].rearrange("p j m r -> p m j r")
@@ -79,13 +82,13 @@ def tile_attend_headpage_proj_kernel(tc, emb_words, emb_scales, wv, base, wo, of
             if h == 0:
                 nc.vector.tensor_copy(got_scales[:], scales[:].indirect(offs_sb[:]))
 
-        wv_codes = keep.tile([P, E], U32, name="wv_codes", align_bytes=64)
-        first_scales = keep.tile([P, P], U8, name="first_scales", align_bytes=64)
-        got_words = keep.tile([P, I], U16, name="got_words", align_bytes=64)
+        wv_codes = sbuf([P, E], U32, "wv_codes")
+        first_scales = sbuf([P, P], U8, "first_scales")
+        got_words = sbuf([P, I], U16, "got_words")
         nc.vector.quantize_mx(out=wv_codes[:, :P].bitcast(FP8X4), scales=first_scales[:],
                               in_=wv_bf[:, 0].rearrange("p m r -> p (m r)"))
         nc.vector.tensor_copy(got_words[:], words[:].indirect(offs_sb[:]))
-        later_scales = keep.tile([P, E - P], U8, name="later_scales", tag="words", align_bytes=64)
+        later_scales = sbuf([P, E - P], U8, "later_scales", tag="words")
         wv_scales = [first_scales[:]] + [later_scales[:, (j - 1) * P : j * P] for j in range(1, PACK)]
         for j in range(1, PACK):
             nc.vector.quantize_mx(out=wv_codes[:, j * P : (j + 1) * P].bitcast(FP8X4), scales=wv_scales[j],
@@ -95,100 +98,111 @@ def tile_attend_headpage_proj_kernel(tc, emb_words, emb_scales, wv, base, wo, of
             nc.tensor.matmul_mx(out=v_ps, lhsT=wv_codes[:, j * P : (j + 1) * P].bitcast(FP8X4), lhsT_scale=wv_scales[j],
                                 rhs=got_words[:].bitcast(FP4X4), rhs_scale=got_scales[:], start=True, stop=True)
 
-        v_sb = keep.tile([P, PACK * I], F32, name="v_sb", align_bytes=64)
+        v_sb = sbuf([P, PACK * I], F32, "v_sb")
         for j in range(2):
-            v_ps = psum.tile([P, I], F32, name="v_ps%d" % j, tag="bank%d" % j)
+            v_ps = bank([P, I], F32, "v_ps%d" % j, j)
             project(j, v_ps[:])
-            nc.vector.tensor_copy(v_sb[:, j * I : (j + 1) * I], v_ps[:])
-        v_ps = psum.tile([P, 2 * I], F32, name="v_ps2", tag="bank2")
+            nc.scalar.copy(v_sb[:, j * I : (j + 1) * I], v_ps[:])
+        v_ps = bank([P, 2 * I], F32, "v_ps2", 2)
         for j in range(2, PACK):
             project(j, v_ps[:, (j - 2) * I : (j - 1) * I])
         nc.scalar.copy(v_sb[:, 2 * I :], v_ps[:])
 
-        wo_bf = [keep.tile([P, F // 2, PACK], BF16, name="wo_bf%d" % h, align_bytes=64) for h in range(2)]
-        for g in range(F // P):
-            nc.scalar.copy(wo_bf[g // 2][:, g % 2 * P : (g % 2 + 1) * P, :].rearrange("p (c i) j -> p c j i", i=4),
-                           wo_raw[:, :, g * P : (g + 1) * P].rearrange("p j (c i) -> p c j i", i=4))
-        wo_codes = keep.tile([P, F], U32, name="wo_codes", align_bytes=64)
+        wo_bf = [sbuf([P, F // 2, PACK], BF16, "wo_bf%d" % h) for h in range(2)]
+        for h in range(2):
+            nc.scalar.copy(wo_bf[h][:].rearrange("p (c i) j -> p c j i", i=4),
+                           wo_raw[:, :, h * F // 2 : (h + 1) * F // 2].rearrange("p j (c i) -> p c j i", i=4))
+        wo_codes = sbuf([P, F], U32, "wo_codes")
         wo_scales = []
 
         def quantise_wo(h, tag):
-            wo_scales.append(keep.tile([P, F // 2], U8, name="wo_scales%d" % h, tag=tag, align_bytes=64))
+            wo_scales.append(sbuf([P, F // 2], U8, "wo_scales%d" % h, tag=tag))
             nc.vector.quantize_mx(out=wo_codes[:, h * F // 2 : (h + 1) * F // 2].bitcast(FP8X4), scales=wo_scales[h][:],
                                   in_=wo_bf[h][:].rearrange("p f j -> p (f j)"))
 
-        x_rows = keep.tile([P, 2, PACK, T_HALF], BF16, name="x_rows", align_bytes=64)
-
-        def add_by_transposes(j, first_place, parts):
-            width = T - first_place
-            blocks = [(slice(c, c + P), slice(first_place + c, first_place + c + P)) for c in range(0, width, P)]
-            turned_ps = psum.tile([P, width], F32, name="turned_ps%d" % j, tag="bank%d" % (4 + j % 2))
-            for b, (cols, places) in enumerate(blocks):
-                nc.tensor.matmul(turned_ps[:, cols], lhsT=base_row(j)[:, places], rhs=ident_f32[:],
-                                 is_transpose=True, start=(b == 0), stop=False)
-            for b, (cols, places) in enumerate(blocks):
-                nc.tensor.matmul(turned_ps[:, cols], lhsT=page[j][:, places], rhs=ident_f32[:],
-                                 is_transpose=True, start=False, stop=(b == len(blocks) - 1))
-            part_width = width // parts
-            turned = [keep.tile([P, part_width], BF16, name="turned%d_%d" % (j, part), tag="turned%d_%d" % (j, part), align_bytes=64)
-                      for part in range(parts)]
-            for part in range(parts):
-                nc.scalar.copy(turned[part][:], turned_ps[:, part * part_width : (part + 1) * part_width])
-            back_ps = psum.tile([P, width], BF16, name="back_ps%d" % j, tag="bank%d" % j)
-            for cols, places in blocks:
-                part, col = divmod(cols.start, part_width)
-                nc.tensor.transpose(back_ps[:, cols], turned[part][:, col : col + P], ident_bf[:])
-            nc.scalar.copy(x_rows[:, first_place // T_HALF :, j, :], back_ps[:].rearrange("p (h t) -> p h t", t=T_HALF))
-
         for j in range(PACK):
             nc.vector.tensor_copy(page[j][:].indirect(offs2_sb[:]), v_sb[:, j * I : (j + 1) * I])
-            if j < LAST - 1:
-                add_by_transposes(j, 0, 1)
-            elif j == LAST - 1:
-                add_by_transposes(j, T_HALF, SCALAR_WEAVES)
-        quantise_wo(0, "wo_scales0")
 
-        x_tags = ["turned%d_%d" % (LAST - 1, c) if c < SCALAR_WEAVES else "x_bf%d" % c for c in range(CHUNKS)]
-        x_bf = [keep.tile([P, T_CHUNK, PACK], BF16, name="x_bf%d" % c, tag=x_tags[c], align_bytes=64) for c in range(CHUNKS)]
-        x_codes = [keep.tile([P, T_CHUNK], U32, name="x_codes%d" % c, align_bytes=64) for c in range(CHUNKS)]
-        x_scales = [keep.tile([P, T_CHUNK], U8, name="x_scales%d" % c, align_bytes=64) for c in range(CHUNKS)]
+        def turned_sums(u, groups):
+            sums = [bank([P, len(chunks), 2, P], F32, "sums%d_%d" % (u, chunks[0]), b) for chunks, b in groups]
+            sources = [(e, base_row(2 * u + e)) for e in range(2)] + [(e, page[2 * u + e]) for e in range(2)]
+            for at, (e, row) in enumerate(sources):
+                for held, (chunks, b) in zip(sums, groups):
+                    for n, c in enumerate(chunks):
+                        nc.tensor.matmul(held[:, n, e, :], lhsT=row[:, c * P : (c + 1) * P], rhs=ident_f32[:], is_transpose=True,
+                                         start=(at == 0 and n == 0), stop=(at == len(sources) - 1 and n == len(chunks) - 1))
+            return sums
+
+        def round_pairs(sums, name):
+            n = sums.shape[1]
+            pairs = sbuf([P, n, P, 2], BF16, name)
+            nc.scalar.copy(pairs[:], sums.rearrange("t n e p -> t n p e"))
+            return pairs
+
+        def turn_back(pairs, n, into):
+            nc.tensor.transpose(into, pairs[:, n].rearrange("t p e -> t (p e)").bitcast(F32), ident_f32[:])
+
+        sums_0, sums_a, sums_b = turned_sums(0, [([0], 3), ([1], 4), ([2, 3], 5)])
+        first_turned = sbuf([P, 2, P], BF16, "first_turned")
+        nc.scalar.copy(first_turned[:], sums_0[:, 0])
+        pairs_a = round_pairs(sums_a[:], "pairs_a")
+        pairs_b = round_pairs(sums_b[:], "pairs_b")
+        first_back = bank([P, 2, P], BF16, "first_back", 0)
+        for e in range(2):
+            nc.tensor.transpose(first_back[:, e, :], first_turned[:, e, :], ident_bf[:])
+        words_1 = bank([P, 2, P], F32, "words_1", 2)
+        words_23 = bank([P, 2, 2, P], F32, "words_23", 1)
+        turn_back(pairs_a, 0, words_1[:, 0, :])
+        for n in range(2):
+            turn_back(pairs_b, n, words_23[:, n, 0, :])
+        x_rows = sbuf([P, PACK, P], BF16, "x_rows")
+        nc.scalar.copy(x_rows[:, :2, :], first_back[:])
+
+        sums_c, sums_d = turned_sums(1, [([1], 3), ([2, 3], 4)])
+        for j in range(2, PACK):
+            nc.vector.tensor_tensor(x_rows[:, j, :], page[j][:, :P], base_row(j)[:, :P], ADD)
+        quantise_wo(0, "base_sb1")
+        x_bf = [sbuf([P, P, PACK], BF16, "x_bf%d" % c) for c in range(CHUNKS)]
+        nc.vector.tensor_copy(x_bf[0][:].rearrange("p (c i) j -> p c j i", i=4), x_rows[:].rearrange("p j (c i) -> p c j i", i=4))
+        quantise_wo(1, "x_rows")
+        pairs_c = round_pairs(sums_c[:], "pairs_c")
+        pairs_d = round_pairs(sums_d[:], "pairs_d")
+        turn_back(pairs_c, 0, words_1[:, 1, :])
+        for n in range(2):
+            turn_back(pairs_d, n, words_23[:, n, 1, :])
+
+        def weave(copy, c, held):
+            copy(x_bf[c][:].rearrange("p t j -> p (t j)").bitcast(F32).rearrange("p (t u) -> p t u", u=2), held.rearrange("p u t -> p t u"))
+
+        x_codes = sbuf([P, T], U32, "x_codes")
+        x_scales = sbuf([P, T], U8, "x_scales")
         out_rows = out.rearrange("(g p) t -> p g t", p=P)
-        y_banks = (6, 0, 4, 2)
 
-        def add_on_vector(j, h):
-            places = slice(h * T_HALF, (h + 1) * T_HALF)
-            nc.vector.tensor_tensor(x_rows[:, h, j, :], page[j][:, places], base_row(j)[:, places], ADD)
-
-        def weave(c):
-            half, at = divmod(c * T_CHUNK, T_HALF)
-            copy = nc.scalar.copy if c < SCALAR_WEAVES else nc.vector.tensor_copy
-            copy(x_bf[c][:].rearrange("p (c i) j -> p c j i", i=4),
-                 x_rows[:, half, :, at : at + T_CHUNK].rearrange("p j (c i) -> p c j i", i=4))
-
-        def multiply(c):
-            places = slice(c * T_CHUNK, (c + 1) * T_CHUNK)
-            nc.vector.quantize_mx(out=x_codes[c][:].bitcast(FP8X4), scales=x_scales[c][:],
+        def quantise_x(c):
+            nc.vector.quantize_mx(out=x_codes[:, c * P : (c + 1) * P].bitcast(FP8X4), scales=x_scales[:, c * P : (c + 1) * P],
                                   in_=x_bf[c][:].rearrange("p t j -> p (t j)"))
-            if c == 0:
-                quantise_wo(1, x_tags[0])
-            for h in range(2):
-                y_ps = psum.tile([P, 2, T_CHUNK], F32, name="y_ps%d_%d" % (c, h), tag="bank%d" % (y_banks[c] + h))
-                for g in range(2):
-                    cols = slice((2 * h + g) * P, (2 * h + g + 1) * P)
-                    nc.tensor.matmul_mx(out=y_ps[:, g, :], lhsT=wo_codes[:, cols].bitcast(FP8X4), lhsT_scale=wo_scales[h][:, g * P : (g + 1) * P],
-                                        rhs=x_codes[c][:].bitcast(FP8X4), rhs_scale=x_scales[c][:], start=True, stop=True)
-                y_sb = keep.tile([P, 2, T_CHUNK], F32, name="y_sb%d_%d" % (c, h), align_bytes=64)
-                if h == 1 and c >= CHUNKS - SHARED_COPIES:
-                    nc.vector.tensor_copy(y_sb[:], y_ps[:])
-                else:
-                    nc.scalar.copy(y_sb[:], y_ps[:])
-                nc.sync.dma_start(out_rows[:, 2 * h : 2 * h + 2, places], y_sb[:])
 
-        add_on_vector(LAST - 1, 0)
-        add_on_vector(LAST, 0)
-        add_on_vector(LAST, 1)
-        for step in range(CHUNKS + 1):
-            if step < CHUNKS:
-                weave(step)
-            if step >= 1:
-                multiply(step - 1)
+        def multiply(groups, places, b, copy):
+            width = places.stop - places.start
+            y_ps = bank([P, len(groups), width], F32, "y_ps%d_%d" % (groups[0], places.start), b)
+            for n, g in enumerate(groups):
+                nc.tensor.matmul_mx(out=y_ps[:, n, :], lhsT=wo_codes[:, g * P : (g + 1) * P].bitcast(FP8X4),
+                                    lhsT_scale=wo_scales[g // 2][:, g % 2 * P : (g % 2 + 1) * P],
+                                    rhs=x_codes[:, places].bitcast(FP8X4), rhs_scale=x_scales[:, places], start=True, stop=True)
+            y_sb = sbuf([P, len(groups), width], F32, "y_sb%d_%d" % (groups[0], places.start))
+            copy(y_sb[:], y_ps[:])
+            nc.sync.dma_start(out_rows[:, groups[0] : groups[-1] + 1, places], y_sb[:])
+
+        quantise_x(0)
+        weave(nc.scalar.copy, 1, words_1[:])
+        multiply([0, 1], slice(0, P), 4, nc.scalar.copy)
+        multiply([2, 3], slice(0, P), 2, nc.scalar.copy)
+        weave(nc.vector.tensor_copy, 2, words_23[:, 0])
+        quantise_x(1)
+        weave(nc.vector.tensor_copy, 3, words_23[:, 1])
+        multiply([0, 1], slice(P, 2 * P), 7, nc.scalar.copy)
+        multiply([2, 3], slice(P, 2 * P), 0, nc.scalar.copy)
+        quantise_x(2)
+        quantise_x(3)
+        for g in range(PACK):
+            multiply([g], slice(2 * P, T), (5, 3, 6, 4)[g], nc.scalar.copy if g % 2 else nc.vector.tensor_copy)

@@ -21,10 +21,9 @@ PACK = 4
 LIST_ROWS = 16
 QUADRANT = 32
 SCALE_ROWS = K // 32
-M_HALF = P // 2
-M_VECTOR = (16, 36)
+M_VECTOR = (32, 84)
 CHUNKS = T // P
-BANK = 512
+ROWS = (2, 3, 1, 0)
 
 
 def tile_attend_headpage_proj_kernel(tc, emb_words, emb_scales, wv, base, wo, offs, offs2, out):
@@ -43,28 +42,27 @@ def tile_attend_headpage_proj_kernel(tc, emb_words, emb_scales, wv, base, wo, of
         offs2_sb = keep.tile([P, I // LIST_ROWS], U16, name="offs2_sb")
         words = sbuf([P, U], U16, "words")
         scales = sbuf([P, U], U8, "scales")
-        wv_raw = [sbuf([P, PACK, E // 2], F32, "wv_raw%d" % h) for h in range(2)]
+        wv_raw = [sbuf([P, 2, E], F32, "wv_raw%d" % h) for h in range(2)]
         base_sb = [sbuf([P, 2, T], F32, "base_sb%d" % u) for u in range(2)]
-        wo_raw = sbuf([P, PACK, F], F32, "wo_raw")
+        wo_raw = [sbuf([P, PACK, F // 2], F32, "wo_raw%d" % h) for h in range(2)]
         page = [sbuf([P, T], F32, "page%d" % j) for j in range(PACK)]
         ident_f32 = sbuf([P, P], F32, "ident_f32")
-        ident_bf = sbuf([P, P], BF16, "ident_bf")
 
         nc.vector.memset(scales[:].bitcast(I32), 0)
         make_identity(nc, ident_f32[:])
-        make_identity(nc, ident_bf[:])
         wv_rows = wv.rearrange("(p r) e -> p r e", r=PACK)
-        nc.sync.dma_start(wv_raw[0][:], wv_rows[:, :, : E // 2])
+        nc.sync.dma_start(wv_raw[0][:], wv_rows[:, :2, :])
         nc.sync.dma_start(offs_sb[:], offs)
         for r in range(4):
             nc.sync.dma_start(scales[r:P:QUADRANT, :].bitcast(I32), emb_scales[0, r:SCALE_ROWS:4, :].bitcast(I32))
-        nc.sync.dma_start(wv_raw[1][:], wv_rows[:, :, E // 2 :])
+        nc.sync.dma_start(wv_raw[1][:], wv_rows[:, 2:, :])
         nc.sync.dma_start(words[:].bitcast(I32), emb_words[0].bitcast(I32))
         nc.sync.dma_start(offs2_sb[:], offs2)
-        nc.sync.dma_start(wo_raw[:], wo.rearrange("(p j) f -> p j f", j=PACK))
+        wo_rows = wo.rearrange("(p j) f -> p j f", j=PACK)
         base_rows = base.rearrange("(p j) t -> p j t", j=PACK)
         for u in range(2):
             nc.sync.dma_start(base_sb[u][:], base_rows[:, 2 * u : 2 * u + 2, :])
+            nc.sync.dma_start(wo_raw[u][:], wo_rows[:, :, u * F // 2 : (u + 1) * F // 2])
         for j in range(PACK):
             nc.vector.memset(page[j][:], 0.0)
 
@@ -76,7 +74,7 @@ def tile_attend_headpage_proj_kernel(tc, emb_words, emb_scales, wv, base, wo, of
         wv_bf = sbuf([P, PACK, P, PACK], BF16, "wv_bf")
         for h in range(2):
             src = wv_raw[h][:].rearrange("p r (m j) -> p m j r", j=PACK)
-            dst = wv_bf[:, :, h * M_HALF : (h + 1) * M_HALF, :].rearrange("p j m r -> p m j r")
+            dst = wv_bf[:, :, :, 2 * h : 2 * h + 2].rearrange("p j m r -> p m j r")
             nc.scalar.copy(dst[:, M_VECTOR[h] :], src[:, M_VECTOR[h] :])
             nc.vector.tensor_copy(dst[:, : M_VECTOR[h]], src[:, : M_VECTOR[h]])
             if h == 0:
@@ -85,94 +83,104 @@ def tile_attend_headpage_proj_kernel(tc, emb_words, emb_scales, wv, base, wo, of
         wv_codes = sbuf([P, E], U32, "wv_codes")
         first_scales = sbuf([P, P], U8, "first_scales")
         got_words = sbuf([P, I], U16, "got_words")
-        nc.vector.quantize_mx(out=wv_codes[:, :P].bitcast(FP8X4), scales=first_scales[:],
-                              in_=wv_bf[:, 0].rearrange("p m r -> p (m r)"))
+        wv_scales = {}
+
+        def quantise_wv(j, plane):
+            wv_scales[j] = plane
+            nc.vector.quantize_mx(out=wv_codes[:, j * P : (j + 1) * P].bitcast(FP8X4), scales=plane,
+                                  in_=wv_bf[:, j].rearrange("p m r -> p (m r)"))
+
+        quantise_wv(ROWS[0], first_scales[:])
         nc.vector.tensor_copy(got_words[:], words[:].indirect(offs_sb[:]))
         later_scales = sbuf([P, E - P], U8, "later_scales", tag="words")
-        wv_scales = [first_scales[:]] + [later_scales[:, (j - 1) * P : j * P] for j in range(1, PACK)]
-        for j in range(1, PACK):
-            nc.vector.quantize_mx(out=wv_codes[:, j * P : (j + 1) * P].bitcast(FP8X4), scales=wv_scales[j],
-                                  in_=wv_bf[:, j].rearrange("p m r -> p (m r)"))
+        for at, j in enumerate(ROWS[1:]):
+            quantise_wv(j, later_scales[:, at * P : (at + 1) * P])
 
         def project(j, v_ps):
             nc.tensor.matmul_mx(out=v_ps, lhsT=wv_codes[:, j * P : (j + 1) * P].bitcast(FP8X4), lhsT_scale=wv_scales[j],
                                 rhs=got_words[:].bitcast(FP4X4), rhs_scale=got_scales[:], start=True, stop=True)
 
-        v_sb = sbuf([P, PACK * I], F32, "v_sb")
-        for j in range(2):
-            v_ps = bank([P, I], F32, "v_ps%d" % j, j)
-            project(j, v_ps[:])
-            nc.scalar.copy(v_sb[:, j * I : (j + 1) * I], v_ps[:])
-        v_ps = bank([P, 2 * I], F32, "v_ps2", 2)
-        for j in range(2, PACK):
-            project(j, v_ps[:, (j - 2) * I : (j - 1) * I])
-        nc.scalar.copy(v_sb[:, 2 * I :], v_ps[:])
+        v_sb = sbuf([P, PACK, I], F32, "v_sb")
+        for at in range(2):
+            v_ps = bank([P, I], F32, "v_ps%d" % at, at)
+            project(ROWS[at], v_ps[:])
+            nc.scalar.copy(v_sb[:, at], v_ps[:])
+        v_ps = bank([P, 2, I], F32, "v_ps2", 2)
+        for at in range(2, PACK):
+            project(ROWS[at], v_ps[:, at - 2])
+        nc.scalar.copy(v_sb[:, 2:], v_ps[:])
 
         wo_bf = [sbuf([P, F // 2, PACK], BF16, "wo_bf%d" % h) for h in range(2)]
         for h in range(2):
             nc.scalar.copy(wo_bf[h][:].rearrange("p (c i) j -> p c j i", i=4),
-                           wo_raw[:, :, h * F // 2 : (h + 1) * F // 2].rearrange("p j (c i) -> p c j i", i=4))
+                           wo_raw[h][:].rearrange("p j (c i) -> p c j i", i=4))
         wo_codes = sbuf([P, F], U32, "wo_codes")
-        wo_scales = []
+        wo_scales = {}
 
-        def quantise_wo(h, tag):
-            wo_scales.append(sbuf([P, F // 2], U8, "wo_scales%d" % h, tag=tag))
-            nc.vector.quantize_mx(out=wo_codes[:, h * F // 2 : (h + 1) * F // 2].bitcast(FP8X4), scales=wo_scales[h][:],
-                                  in_=wo_bf[h][:].rearrange("p f j -> p (f j)"))
+        def quantise_wo(first, last, tag):
+            plane = sbuf([P, (last + 1 - first) * P], U8, "wo_scales%d" % first, tag=tag)
+            for g in range(first, last + 1):
+                wo_scales[g] = plane[:, (g - first) * P : (g - first + 1) * P]
+            nc.vector.quantize_mx(out=wo_codes[:, first * P : (last + 1) * P].bitcast(FP8X4), scales=plane[:],
+                                  in_=wo_bf[first // 2][:, first % 2 * P : (last % 2 + 1) * P].rearrange("p f j -> p (f j)"))
 
-        for j in range(PACK):
-            nc.vector.tensor_copy(page[j][:].indirect(offs2_sb[:]), v_sb[:, j * I : (j + 1) * I])
+        for at, j in enumerate(ROWS):
+            nc.vector.tensor_copy(page[j][:].indirect(offs2_sb[:]), v_sb[:, at])
 
-        def turned_sums(u, groups):
-            sums = [bank([P, len(chunks), 2, P], F32, "sums%d_%d" % (u, chunks[0]), b) for chunks, b in groups]
-            sources = [(e, base_row(2 * u + e)) for e in range(2)] + [(e, page[2 * u + e]) for e in range(2)]
-            for at, (e, row) in enumerate(sources):
-                for held, (chunks, b) in zip(sums, groups):
+        def turn(sums, u, source, ident, start, stop):
+            for at, e in enumerate((0, 1) if u else (1, 0)):
+                for held, chunks in sums:
                     for n, c in enumerate(chunks):
-                        nc.tensor.matmul(held[:, n, e, :], lhsT=row[:, c * P : (c + 1) * P], rhs=ident_f32[:], is_transpose=True,
-                                         start=(at == 0 and n == 0), stop=(at == len(sources) - 1 and n == len(chunks) - 1))
-            return sums
+                        nc.tensor.matmul(held[:, n, e, :], lhsT=source(2 * u + e)[:, c * P : (c + 1) * P], rhs=ident[:], is_transpose=True,
+                                         start=start and at == 0 and n == 0, stop=stop and at == 1 and n == len(chunks) - 1)
+
+        def sum_banks(name, groups):
+            return [(bank([P, len(chunks), 2, P], F32, "%s%d" % (name, b), b), chunks) for b, chunks in groups]
 
         def round_pairs(sums, name):
-            n = sums.shape[1]
-            pairs = sbuf([P, n, P, 2], BF16, name)
-            nc.scalar.copy(pairs[:], sums.rearrange("t n e p -> t n p e"))
+            pairs = sbuf([P, sums.shape[1], P, 2], BF16, name)
+            nc.scalar.copy(pairs[:], sums[:].rearrange("t n e p -> t n p e"))
             return pairs
 
         def turn_back(pairs, n, into):
             nc.tensor.transpose(into, pairs[:, n].rearrange("t p e -> t (p e)").bitcast(F32), ident_f32[:])
 
-        sums_0, sums_a, sums_b = turned_sums(0, [([0], 3), ([1], 4), ([2, 3], 5)])
-        first_turned = sbuf([P, 2, P], BF16, "first_turned")
-        nc.scalar.copy(first_turned[:], sums_0[:, 0])
-        pairs_a = round_pairs(sums_a[:], "pairs_a")
-        pairs_b = round_pairs(sums_b[:], "pairs_b")
-        first_back = bank([P, 2, P], BF16, "first_back", 0)
-        for e in range(2):
-            nc.tensor.transpose(first_back[:, e, :], first_turned[:, e, :], ident_bf[:])
-        words_1 = bank([P, 2, P], F32, "words_1", 2)
-        words_23 = bank([P, 2, 2, P], F32, "words_23", 1)
-        turn_back(pairs_a, 0, words_1[:, 0, :])
-        for n in range(2):
-            turn_back(pairs_b, n, words_23[:, n, 0, :])
-        x_rows = sbuf([P, PACK, P], BF16, "x_rows")
-        nc.scalar.copy(x_rows[:, :2, :], first_back[:])
-
-        sums_c, sums_d = turned_sums(1, [([1], 3), ([2, 3], 4)])
-        for j in range(2, PACK):
-            nc.vector.tensor_tensor(x_rows[:, j, :], page[j][:, :P], base_row(j)[:, :P], ADD)
-        quantise_wo(0, "base_sb1")
+        FIRST = CHUNKS - 1
+        early = sum_banks("early", [(3, [FIRST, 0]), (4, [1, 2])])
+        late = sum_banks("late", [(5, [0]), (6, [1, 2])])
+        turn(late, 0, base_row, ident_f32, True, False)
+        turn(early, 1, base_row, ident_f32, True, False)
+        turn(early, 1, lambda j: page[j], ident_f32, False, True)
+        words_a = bank([P, 3, P], F32, "words_a", 7)
+        words_b = bank([P, 2, 2, P], F32, "words_b", 0)
+        held = [words_a[:, :2], words_b[:, 0], words_b[:, 1]]
         x_bf = [sbuf([P, P, PACK], BF16, "x_bf%d" % c) for c in range(CHUNKS)]
-        nc.vector.tensor_copy(x_bf[0][:].rearrange("p (c i) j -> p c j i", i=4), x_rows[:].rearrange("p j (c i) -> p c j i", i=4))
-        quantise_wo(1, "x_rows")
-        pairs_c = round_pairs(sums_c[:], "pairs_c")
-        pairs_d = round_pairs(sums_d[:], "pairs_d")
-        turn_back(pairs_c, 0, words_1[:, 1, :])
+        x_words = [x_bf[c][:].rearrange("p t j -> p (t j)").bitcast(F32).rearrange("p (t u) -> p t u", u=2) for c in range(CHUNKS)]
+        pairs_a = round_pairs(early[0][0], "pairs_a")
+        pairs_b = round_pairs(early[1][0], "pairs_b")
+        turn_back(pairs_a, 0, words_a[:, 2])
+        turn_back(pairs_a, 1, held[0][:, 1])
         for n in range(2):
-            turn_back(pairs_d, n, words_23[:, n, 1, :])
+            turn_back(pairs_b, n, held[1 + n][:, 1])
+        late_ident = sbuf([P, P], F32, "late_ident", tag="pairs_a")
+        nc.scalar.copy(late_ident[:], ident_f32[:])
+        nc.scalar.copy(x_words[FIRST][:, :, 1], words_a[:, 2])
+        turn(late, 0, lambda j: page[j], late_ident, False, True)
 
-        def weave(copy, c, held):
-            copy(x_bf[c][:].rearrange("p t j -> p (t j)").bitcast(F32).rearrange("p (t u) -> p t u", u=2), held.rearrange("p u t -> p t u"))
+        x_rows = sbuf([P, 2, P], BF16, "x_rows")
+        for j in (1, 0):
+            nc.vector.tensor_tensor(x_rows[:, j, :], page[j][:, FIRST * P :], base_row(j)[:, FIRST * P :], ADD)
+        quantise_wo(0, 0, "base_sb0")
+        nc.vector.tensor_copy(x_bf[FIRST][:, :, :2], x_rows[:].rearrange("p j t -> p t j"))
+        quantise_wo(1, 1, "x_rows")
+        pairs_c = round_pairs(late[0][0], "pairs_c")
+        pairs_d = round_pairs(late[1][0], "pairs_d")
+        turn_back(pairs_c, 0, held[0][:, 0])
+        for n in range(2):
+            turn_back(pairs_d, n, held[1 + n][:, 0])
+
+        def weave(copy, c):
+            copy(x_words[c], held[c].rearrange("p u t -> p t u"))
 
         x_codes = sbuf([P, T], U32, "x_codes")
         x_scales = sbuf([P, T], U8, "x_scales")
@@ -187,22 +195,23 @@ def tile_attend_headpage_proj_kernel(tc, emb_words, emb_scales, wv, base, wo, of
             y_ps = bank([P, len(groups), width], F32, "y_ps%d_%d" % (groups[0], places.start), b)
             for n, g in enumerate(groups):
                 nc.tensor.matmul_mx(out=y_ps[:, n, :], lhsT=wo_codes[:, g * P : (g + 1) * P].bitcast(FP8X4),
-                                    lhsT_scale=wo_scales[g // 2][:, g % 2 * P : (g % 2 + 1) * P],
+                                    lhsT_scale=wo_scales[g],
                                     rhs=x_codes[:, places].bitcast(FP8X4), rhs_scale=x_scales[:, places], start=True, stop=True)
             y_sb = sbuf([P, len(groups), width], F32, "y_sb%d_%d" % (groups[0], places.start))
             copy(y_sb[:], y_ps[:])
             nc.sync.dma_start(out_rows[:, groups[0] : groups[-1] + 1, places], y_sb[:])
 
+        quantise_x(FIRST)
+        quantise_wo(2, 3, "x_bf%d" % FIRST)
+        weave(nc.scalar.copy, 0)
+        multiply([0, 1], slice(FIRST * P, T), 5, nc.scalar.copy)
         quantise_x(0)
-        weave(nc.scalar.copy, 1, words_1[:])
-        multiply([0, 1], slice(0, P), 4, nc.scalar.copy)
-        multiply([2, 3], slice(0, P), 2, nc.scalar.copy)
-        weave(nc.vector.tensor_copy, 2, words_23[:, 0])
+        multiply([2, 3], slice(FIRST * P, T), 7, nc.scalar.copy)
+        weave(nc.vector.tensor_copy, 1)
+        weave(nc.vector.tensor_copy, 2)
+        multiply([0, 1], slice(0, P), 3, nc.scalar.copy)
+        multiply([2, 3], slice(0, P), 4, nc.scalar.copy)
         quantise_x(1)
-        weave(nc.vector.tensor_copy, 3, words_23[:, 1])
-        multiply([0, 1], slice(P, 2 * P), 7, nc.scalar.copy)
-        multiply([2, 3], slice(P, 2 * P), 0, nc.scalar.copy)
         quantise_x(2)
-        quantise_x(3)
         for g in range(PACK):
-            multiply([g], slice(2 * P, T), (5, 3, 6, 4)[g], nc.scalar.copy if g % 2 else nc.vector.tensor_copy)
+            multiply([g], slice(P, FIRST * P), (1, 2, 6, 5)[g], nc.scalar.copy if g % 2 else nc.vector.tensor_copy)

@@ -44,12 +44,14 @@ def tile_attend_headpage_proj_kernel(tc, emb_words, emb_scales, wv, base, wo, of
         scales = sbuf([P, U], U8, "scales")
         wv_raw = [sbuf([P, 2, E], F32, "wv_raw%d" % h) for h in range(2)]
         base_sb = [sbuf([P, 2, T], F32, "base_sb%d" % u) for u in range(2)]
-        wo_raw = [sbuf([P, PACK, F // 2], F32, "wo_raw%d" % h) for h in range(2)]
+        wo_raw = sbuf([P, PACK, F], F32, "wo_raw")
         page = [sbuf([P, T], F32, "page%d" % j) for j in range(PACK)]
         ident_f32 = sbuf([P, P], F32, "ident_f32")
+        ident_bf = sbuf([P, P], BF16, "ident_bf")
 
         nc.vector.memset(scales[:].bitcast(I32), 0)
         make_identity(nc, ident_f32[:])
+        make_identity(nc, ident_bf[:])
         wv_rows = wv.rearrange("(p r) e -> p r e", r=PACK)
         nc.sync.dma_start(wv_raw[0][:], wv_rows[:, :2, :])
         nc.sync.dma_start(offs_sb[:], offs)
@@ -58,11 +60,10 @@ def tile_attend_headpage_proj_kernel(tc, emb_words, emb_scales, wv, base, wo, of
         nc.sync.dma_start(wv_raw[1][:], wv_rows[:, 2:, :])
         nc.sync.dma_start(words[:].bitcast(I32), emb_words[0].bitcast(I32))
         nc.sync.dma_start(offs2_sb[:], offs2)
-        wo_rows = wo.rearrange("(p j) f -> p j f", j=PACK)
+        nc.sync.dma_start(wo_raw[:], wo.rearrange("(p j) f -> p j f", j=PACK))
         base_rows = base.rearrange("(p j) t -> p j t", j=PACK)
-        for u in range(2):
+        for u in (1, 0):
             nc.sync.dma_start(base_sb[u][:], base_rows[:, 2 * u : 2 * u + 2, :])
-            nc.sync.dma_start(wo_raw[u][:], wo_rows[:, :, u * F // 2 : (u + 1) * F // 2])
         for j in range(PACK):
             nc.vector.memset(page[j][:], 0.0)
 
@@ -113,74 +114,53 @@ def tile_attend_headpage_proj_kernel(tc, emb_words, emb_scales, wv, base, wo, of
         wo_bf = [sbuf([P, F // 2, PACK], BF16, "wo_bf%d" % h) for h in range(2)]
         for h in range(2):
             nc.scalar.copy(wo_bf[h][:].rearrange("p (c i) j -> p c j i", i=4),
-                           wo_raw[h][:].rearrange("p j (c i) -> p c j i", i=4))
+                           wo_raw[:, :, h * F // 2 : (h + 1) * F // 2].rearrange("p j (c i) -> p c j i", i=4))
         wo_codes = sbuf([P, F], U32, "wo_codes")
-        wo_scales = {}
-
-        def quantise_wo(first, last, tag):
-            plane = sbuf([P, (last + 1 - first) * P], U8, "wo_scales%d" % first, tag=tag)
-            for g in range(first, last + 1):
-                wo_scales[g] = plane[:, (g - first) * P : (g - first + 1) * P]
-            nc.vector.quantize_mx(out=wo_codes[:, first * P : (last + 1) * P].bitcast(FP8X4), scales=plane[:],
-                                  in_=wo_bf[first // 2][:, first % 2 * P : (last % 2 + 1) * P].rearrange("p f j -> p (f j)"))
 
         for at, j in enumerate(ROWS):
             nc.vector.tensor_copy(page[j][:].indirect(offs2_sb[:]), v_sb[:, at])
 
-        def turn(sums, u, source, ident, start, stop):
-            for at, e in enumerate((0, 1) if u else (1, 0)):
-                for held, chunks in sums:
-                    for n, c in enumerate(chunks):
-                        nc.tensor.matmul(held[:, n, e, :], lhsT=source(2 * u + e)[:, c * P : (c + 1) * P], rhs=ident[:], is_transpose=True,
-                                         start=start and at == 0 and n == 0, stop=stop and at == 1 and n == len(chunks) - 1)
+        x_bf = sbuf([P, T, PACK], BF16, "x_bf")
+        x_words = x_bf[:].rearrange("p t j -> p (t j)").bitcast(F32).rearrange("p (t u) -> p t u", u=2)
+        sums = [bank([P, 2, 2, P], F32, "sums%d" % h, 3 + h) for h in range(2)]
+        for at, row in enumerate([base_row(2), base_row(3), page[2], page[3]]):
+            for c in range(CHUNKS):
+                nc.tensor.matmul(sums[c // 2][:, c % 2, at % 2, :], lhsT=row[:, c * P : (c + 1) * P], rhs=ident_f32[:], is_transpose=True,
+                                 start=at == 0 and c % 2 == 0, stop=at == 3 and c % 2 == 1)
+        pairs = [sbuf([P, 2, P, 2], BF16, "pairs%d" % h) for h in range(2)]
+        for h in range(2):
+            nc.scalar.copy(pairs[h][:], sums[h][:].rearrange("t n e p -> t n p e"))
+        for h in range(2):
+            held = bank([P, 2 * P], F32, "held%d" % h, h)
+            for n in range(2):
+                nc.tensor.transpose(held[:, n * P : (n + 1) * P], pairs[h][:, n].rearrange("t p e -> t (p e)").bitcast(F32), ident_f32[:])
+            nc.scalar.copy(x_words[:, h * 2 * P : (h + 1) * 2 * P, 1], held[:])
 
-        def sum_banks(name, groups):
-            return [(bank([P, len(chunks), 2, P], F32, "%s%d" % (name, b), b), chunks) for b, chunks in groups]
-
-        def round_pairs(sums, name):
-            pairs = sbuf([P, sums.shape[1], P, 2], BF16, name)
-            nc.scalar.copy(pairs[:], sums[:].rearrange("t n e p -> t n p e"))
-            return pairs
-
-        def turn_back(pairs, n, into):
-            nc.tensor.transpose(into, pairs[:, n].rearrange("t p e -> t (p e)").bitcast(F32), ident_f32[:])
-
-        FIRST = CHUNKS - 1
-        early = sum_banks("early", [(3, [FIRST, 0]), (4, [1, 2])])
-        late = sum_banks("late", [(5, [0]), (6, [1, 2])])
-        turn(late, 0, base_row, ident_f32, True, False)
-        turn(early, 1, base_row, ident_f32, True, False)
-        turn(early, 1, lambda j: page[j], ident_f32, False, True)
-        words_a = bank([P, 3, P], F32, "words_a", 7)
-        words_b = bank([P, 2, 2, P], F32, "words_b", 0)
-        held = [words_a[:, :2], words_b[:, 0], words_b[:, 1]]
-        x_bf = [sbuf([P, P, PACK], BF16, "x_bf%d" % c) for c in range(CHUNKS)]
-        x_words = [x_bf[c][:].rearrange("p t j -> p (t j)").bitcast(F32).rearrange("p (t u) -> p t u", u=2) for c in range(CHUNKS)]
-        pairs_a = round_pairs(early[0][0], "pairs_a")
-        pairs_b = round_pairs(early[1][0], "pairs_b")
-        turn_back(pairs_a, 0, words_a[:, 2])
-        turn_back(pairs_a, 1, held[0][:, 1])
+        x_rows = sbuf([P, 2, T], BF16, "x_rows", tag="pairs1")
+        third = bank([P, 2, P], F32, "third", 4)
+        for at, row in enumerate([base_row(1), page[1]]):
+            for n in range(2):
+                nc.tensor.matmul(third[:, n, :], lhsT=row[:, (2 + n) * P : (3 + n) * P], rhs=ident_f32[:], is_transpose=True,
+                                 start=at == 0 and n == 0, stop=at == 1 and n == 1)
+        third_bf = sbuf([P, 2, P], BF16, "third_bf")
+        nc.scalar.copy(third_bf[:], third[:])
+        third_back = bank([P, 2 * P], BF16, "third_back", 5)
         for n in range(2):
-            turn_back(pairs_b, n, held[1 + n][:, 1])
-        late_ident = sbuf([P, P], F32, "late_ident", tag="pairs_a")
-        nc.scalar.copy(late_ident[:], ident_f32[:])
-        nc.scalar.copy(x_words[FIRST][:, :, 1], words_a[:, 2])
-        turn(late, 0, lambda j: page[j], late_ident, False, True)
+            nc.tensor.transpose(third_back[:, n * P : (n + 1) * P], third_bf[:, n], ident_bf[:])
+        nc.scalar.copy(x_rows[:, 1, 2 * P :], third_back[:])
+        wo_scales = sbuf([P, F], U8, "wo_scales", tag="ident_f32")
 
-        x_rows = sbuf([P, 2, P], BF16, "x_rows")
-        for j in (1, 0):
-            nc.vector.tensor_tensor(x_rows[:, j, :], page[j][:, FIRST * P :], base_row(j)[:, FIRST * P :], ADD)
-        quantise_wo(0, 0, "base_sb0")
-        nc.vector.tensor_copy(x_bf[FIRST][:, :, :2], x_rows[:].rearrange("p j t -> p t j"))
-        quantise_wo(1, 1, "x_rows")
-        pairs_c = round_pairs(late[0][0], "pairs_c")
-        pairs_d = round_pairs(late[1][0], "pairs_d")
-        turn_back(pairs_c, 0, held[0][:, 0])
-        for n in range(2):
-            turn_back(pairs_d, n, held[1 + n][:, 0])
+        def quantise_wo(first, last):
+            cols = slice(first * P, (last + 1) * P)
+            nc.vector.quantize_mx(out=wo_codes[:, cols].bitcast(FP8X4), scales=wo_scales[:, cols],
+                                  in_=wo_bf[first // 2][:, first % 2 * P : (last % 2 + 1) * P].rearrange("p f j -> p (f j)"))
+
+        def add(j, first, last):
+            places = slice(first * P, (last + 1) * P)
+            nc.vector.tensor_tensor(x_rows[:, j, places], page[j][:, places], base_row(j)[:, places], ADD)
 
         def weave(copy, c):
-            copy(x_words[c], held[c].rearrange("p u t -> p t u"))
+            copy(x_bf[:, c * P : (c + 1) * P, :2], x_rows[:, :, c * P : (c + 1) * P].rearrange("p j t -> p t j"))
 
         x_codes = sbuf([P, T], U32, "x_codes")
         x_scales = sbuf([P, T], U8, "x_scales")
@@ -188,30 +168,39 @@ def tile_attend_headpage_proj_kernel(tc, emb_words, emb_scales, wv, base, wo, of
 
         def quantise_x(c):
             nc.vector.quantize_mx(out=x_codes[:, c * P : (c + 1) * P].bitcast(FP8X4), scales=x_scales[:, c * P : (c + 1) * P],
-                                  in_=x_bf[c][:].rearrange("p t j -> p (t j)"))
+                                  in_=x_bf[:, c * P : (c + 1) * P].rearrange("p t j -> p (t j)"))
 
         def multiply(groups, places, b, copy):
             width = places.stop - places.start
             y_ps = bank([P, len(groups), width], F32, "y_ps%d_%d" % (groups[0], places.start), b)
             for n, g in enumerate(groups):
                 nc.tensor.matmul_mx(out=y_ps[:, n, :], lhsT=wo_codes[:, g * P : (g + 1) * P].bitcast(FP8X4),
-                                    lhsT_scale=wo_scales[g],
+                                    lhsT_scale=wo_scales[:, g * P : (g + 1) * P],
                                     rhs=x_codes[:, places].bitcast(FP8X4), rhs_scale=x_scales[:, places], start=True, stop=True)
             y_sb = sbuf([P, len(groups), width], F32, "y_sb%d_%d" % (groups[0], places.start))
             copy(y_sb[:], y_ps[:])
             nc.sync.dma_start(out_rows[:, groups[0] : groups[-1] + 1, places], y_sb[:])
 
-        quantise_x(FIRST)
-        quantise_wo(2, 3, "x_bf%d" % FIRST)
-        weave(nc.scalar.copy, 0)
-        multiply([0, 1], slice(FIRST * P, T), 5, nc.scalar.copy)
+        add(1, 0, 0)
+        add(0, 0, 0)
+        add(1, 1, 1)
+        weave(nc.vector.tensor_copy, 0)
+        add(0, 1, 1)
+        weave(nc.scalar.copy, 1)
+        quantise_wo(0, 1)
         quantise_x(0)
-        multiply([2, 3], slice(FIRST * P, T), 7, nc.scalar.copy)
-        weave(nc.vector.tensor_copy, 1)
-        weave(nc.vector.tensor_copy, 2)
-        multiply([0, 1], slice(0, P), 3, nc.scalar.copy)
-        multiply([2, 3], slice(0, P), 4, nc.scalar.copy)
+        add(0, 2, 3)
         quantise_x(1)
+        multiply([0, 1], slice(0, P), 4, nc.scalar.copy)
+        quantise_wo(2, 3)
+        multiply([0, 1], slice(P, 2 * P), 2, nc.scalar.copy)
+        weave(nc.vector.tensor_copy, 2)
+        weave(nc.vector.tensor_copy, 3)
+        multiply([2, 3], slice(0, P), 6, nc.scalar.copy)
+        multiply([2, 3], slice(P, 2 * P), 7, nc.scalar.copy)
         quantise_x(2)
-        for g in range(PACK):
-            multiply([g], slice(P, FIRST * P), (1, 2, 6, 5)[g], nc.scalar.copy if g % 2 else nc.vector.tensor_copy)
+        quantise_x(3)
+        multiply([0, 1], slice(2 * P, 3 * P), 3, nc.vector.tensor_copy)
+        multiply([2, 3], slice(2 * P, 3 * P), 5, nc.scalar.copy)
+        multiply([0, 1], slice(3 * P, T), 0, nc.vector.tensor_copy)
+        multiply([2, 3], slice(3 * P, T), 1, nc.scalar.copy)

@@ -21,6 +21,7 @@ PACK = 4
 LIST_ROWS = 16
 QUADRANT = 32
 SCALE_ROWS = K // 32
+SCALE_AT = P - SCALE_ROWS
 M_VECTOR = (32, 84)
 CHUNKS = T // P
 ROWS = (2, 3, 1, 0)
@@ -43,34 +44,35 @@ def tile_attend_headpage_proj_kernel(tc, emb_words, emb_scales, wv, base, wo, of
         words = sbuf([P, U], U16, "words")
         scales = sbuf([P, U], U8, "scales")
         wv_raw = [sbuf([P, 2, E], F32, "wv_raw%d" % h) for h in range(2)]
-        base_sb = [sbuf([P, 2, T], F32, "base_sb%d" % u) for u in range(2)]
-        wo_raw = sbuf([P, PACK, F], F32, "wo_raw")
         page = [sbuf([P, T], F32, "page%d" % j) for j in range(PACK)]
         ident_f32 = sbuf([P, P], F32, "ident_f32")
         ident_bf = sbuf([P, P], BF16, "ident_bf")
 
-        nc.vector.memset(scales[:].bitcast(I32), 0)
+        nc.vector.memset(scales[:SCALE_AT].bitcast(I32), 0)
+        got_scales = sbuf([P, I], U8, "got_scales")
+        nc.vector.memset(got_scales[:].bitcast(I32), 0)
         make_identity(nc, ident_f32[:])
         make_identity(nc, ident_bf[:])
         wv_rows = wv.rearrange("(p r) e -> p r e", r=PACK)
-        nc.sync.dma_start(wv_raw[0][:], wv_rows[:, :2, :])
         nc.sync.dma_start(offs_sb[:], offs)
-        for r in range(4):
-            nc.sync.dma_start(scales[r:P:QUADRANT, :].bitcast(I32), emb_scales[0, r:SCALE_ROWS:4, :].bitcast(I32))
-        nc.sync.dma_start(wv_raw[1][:], wv_rows[:, 2:, :])
-        nc.sync.dma_start(words[:].bitcast(I32), emb_words[0].bitcast(I32))
+        nc.sync.dma_start(scales[SCALE_AT:, :].bitcast(I32), emb_scales[0].bitcast(I32))
         nc.sync.dma_start(offs2_sb[:], offs2)
-        nc.sync.dma_start(wo_raw[:], wo.rearrange("(p j) f -> p j f", j=PACK))
+        nc.scalar.dma_start(wv_raw[0][:], wv_rows[:, :2, :])
+        nc.scalar.dma_start(wv_raw[1][:], wv_rows[:, 2:, :])
+        nc.scalar.dma_start(words[:].bitcast(I32), emb_words[0].bitcast(I32))
         base_rows = base.rearrange("(p j) t -> p j t", j=PACK)
-        for u in (1, 0):
-            nc.sync.dma_start(base_sb[u][:], base_rows[:, 2 * u : 2 * u + 2, :])
+        got_rows = sbuf([P, I], U8, "got_rows")
+        nc.vector.tensor_copy(got_rows[:], scales[:].indirect(offs_sb[:]))
+        for q in range(4):
+            nc.sync.dma_start(got_scales[QUADRANT * q : QUADRANT * q + 4, :].bitcast(I32),
+                              got_rows[SCALE_AT + 4 * q : SCALE_AT + 4 * q + 4, :].bitcast(I32))
+        wo_raw = sbuf([P, PACK, F], F32, "wo_raw", tag="scales")
+        nc.sync.dma_start(wo_raw[:], wo.rearrange("(p j) f -> p j f", j=PACK))
         for j in range(PACK):
             nc.vector.memset(page[j][:], 0.0)
 
         def base_row(j):
             return base_sb[j // 2][:, j % 2, :]
-
-        got_scales = sbuf([P, I], U8, "got_scales")
 
         wv_bf = sbuf([P, PACK, P, PACK], BF16, "wv_bf")
         for h in range(2):
@@ -78,8 +80,11 @@ def tile_attend_headpage_proj_kernel(tc, emb_words, emb_scales, wv, base, wo, of
             dst = wv_bf[:, :, :, 2 * h : 2 * h + 2].rearrange("p j m r -> p m j r")
             nc.scalar.copy(dst[:, M_VECTOR[h] :], src[:, M_VECTOR[h] :])
             nc.vector.tensor_copy(dst[:, : M_VECTOR[h]], src[:, : M_VECTOR[h]])
-            if h == 0:
-                nc.vector.tensor_copy(got_scales[:], scales[:].indirect(offs_sb[:]))
+
+        base_sb = {}
+        for h, u in enumerate((1, 0)):
+            base_sb[u] = sbuf([P, 2, T], F32, "base_sb%d" % u, tag="wv_raw%d" % h)
+            nc.sync.dma_start(base_sb[u][:], base_rows[:, 2 * u : 2 * u + 2, :])
 
         wv_codes = sbuf([P, E], U32, "wv_codes")
         first_scales = sbuf([P, P], U8, "first_scales")
@@ -96,6 +101,7 @@ def tile_attend_headpage_proj_kernel(tc, emb_words, emb_scales, wv, base, wo, of
         later_scales = sbuf([P, E - P], U8, "later_scales", tag="words")
         for at, j in enumerate(ROWS[1:]):
             quantise_wv(j, later_scales[:, at * P : (at + 1) * P])
+
 
         def project(j, v_ps):
             nc.tensor.matmul_mx(out=v_ps, lhsT=wv_codes[:, j * P : (j + 1) * P].bitcast(FP8X4), lhsT_scale=wv_scales[j],

@@ -54,12 +54,12 @@ def tile_attend_headpage_proj_kernel(tc, emb_words, emb_scales, wv, base, wo, of
         make_identity(nc, ident_f32[:])
         make_identity(nc, ident_bf[:])
         wv_rows = wv.rearrange("(p r) e -> p r e", r=PACK)
-        nc.sync.dma_start(offs_sb[:], offs)
         nc.sync.dma_start(scales[SCALE_AT:, :].bitcast(I32), emb_scales[0].bitcast(I32))
+        nc.sync.dma_start(offs_sb[:], offs)
+        nc.sync.dma_start(wv_raw[0][:], wv_rows[:, :2, :])
+        nc.sync.dma_start(wv_raw[1][:], wv_rows[:, 2:, :])
+        nc.sync.dma_start(words[:].bitcast(I32), emb_words[0].bitcast(I32))
         nc.sync.dma_start(offs2_sb[:], offs2)
-        nc.scalar.dma_start(wv_raw[0][:], wv_rows[:, :2, :])
-        nc.scalar.dma_start(wv_raw[1][:], wv_rows[:, 2:, :])
-        nc.scalar.dma_start(words[:].bitcast(I32), emb_words[0].bitcast(I32))
         base_rows = base.rearrange("(p j) t -> p j t", j=PACK)
         got_rows = sbuf([P, I], U8, "got_rows")
         nc.vector.tensor_copy(got_rows[:], scales[:].indirect(offs_sb[:]))

@@ -103,15 +103,16 @@ def tile_attend_headpage_proj_kernel(tc, emb_words, emb_scales, wv, base, wo, of
             quantise_wv(j, later_scales[:, at * P : (at + 1) * P])
 
 
-        def project(j, v_ps):
+        def project(j, v_ps, slots=slice(0, I)):
             nc.tensor.matmul_mx(out=v_ps, lhsT=wv_codes[:, j * P : (j + 1) * P].bitcast(FP8X4), lhsT_scale=wv_scales[j],
-                                rhs=got_words[:].bitcast(FP4X4), rhs_scale=got_scales[:], start=True, stop=True)
+                                rhs=got_words[:, slots].bitcast(FP4X4), rhs_scale=got_scales[:, slots], start=True, stop=True)
 
         v_sb = sbuf([P, PACK, I], F32, "v_sb")
-        for at in range(2):
-            v_ps = bank([P, I], F32, "v_ps%d" % at, at)
-            project(ROWS[at], v_ps[:])
-            nc.scalar.copy(v_sb[:, at], v_ps[:])
+        pieces = [(0, slice(0, I // 2)), (1, slice(0, I)), (0, slice(I // 2, I))]
+        for b, (at, slots) in zip((0, 1, 7), pieces):
+            v_ps = bank([P, slots.stop - slots.start], F32, "v_ps%d" % b, b)
+            project(ROWS[at], v_ps[:], slots)
+            nc.scalar.copy(v_sb[:, at, slots], v_ps[:])
         v_ps = bank([P, 2, I], F32, "v_ps2", 2)
         for at in range(2, PACK):
             project(ROWS[at], v_ps[:, at - 2])
@@ -123,8 +124,8 @@ def tile_attend_headpage_proj_kernel(tc, emb_words, emb_scales, wv, base, wo, of
                            wo_raw[:, :, h * F // 2 : (h + 1) * F // 2].rearrange("p j (c i) -> p c j i", i=4))
         wo_codes = sbuf([P, F], U32, "wo_codes")
 
-        for at, j in enumerate(ROWS):
-            nc.vector.tensor_copy(page[j][:].indirect(offs2_sb[:]), v_sb[:, at])
+        for at, slots in pieces + [(2, slice(0, I)), (3, slice(0, I))]:
+            nc.vector.tensor_copy(page[ROWS[at]][:].indirect(offs2_sb[:, slots.start // LIST_ROWS : slots.stop // LIST_ROWS]), v_sb[:, at, slots])
 
         x_bf = sbuf([P, T, PACK], BF16, "x_bf")
         x_words = x_bf[:].rearrange("p t j -> p (t j)").bitcast(F32).rearrange("p (t u) -> p t u", u=2)
@@ -136,20 +137,24 @@ def tile_attend_headpage_proj_kernel(tc, emb_words, emb_scales, wv, base, wo, of
         pairs = [sbuf([P, 2, P, 2], BF16, "pairs%d" % h) for h in range(2)]
         for h in range(2):
             nc.scalar.copy(pairs[h][:], sums[h][:].rearrange("t n e p -> t n p e"))
-        for h in range(2):
+
+        def lay_pairs(h):
             held = bank([P, 2 * P], F32, "held%d" % h, h)
             for n in range(2):
                 nc.tensor.transpose(held[:, n * P : (n + 1) * P], pairs[h][:, n].rearrange("t p e -> t (p e)").bitcast(F32), ident_f32[:])
-            nc.scalar.copy(x_words[:, h * 2 * P : (h + 1) * 2 * P, 1], held[:])
+            nc.scalar.copy(x_words[:, h * 2 * P : (h + 1) * 2 * P, :], held[:].unsqueeze(2).to_broadcast([P, 2 * P, 2]))
 
-        x_rows = sbuf([P, 2, T], BF16, "x_rows", tag="pairs1")
-        third = bank([P, 2, P], F32, "third", 4)
+        lay_pairs(0)
+        third = bank([P, 2, P], F32, "third", 6)
         for at, row in enumerate([base_row(1), page[1]]):
             for n in range(2):
                 nc.tensor.matmul(third[:, n, :], lhsT=row[:, (2 + n) * P : (3 + n) * P], rhs=ident_f32[:], is_transpose=True,
                                  start=at == 0 and n == 0, stop=at == 1 and n == 1)
         third_bf = sbuf([P, 2, P], BF16, "third_bf")
         nc.scalar.copy(third_bf[:], third[:])
+        lay_pairs(1)
+
+        x_rows = sbuf([P, 2, T], BF16, "x_rows", tag="pairs1")
         third_back = bank([P, 2 * P], BF16, "third_back", 5)
         for n in range(2):
             nc.tensor.transpose(third_back[:, n * P : (n + 1) * P], third_bf[:, n], ident_bf[:])
@@ -187,6 +192,9 @@ def tile_attend_headpage_proj_kernel(tc, emb_words, emb_scales, wv, base, wo, of
             copy(y_sb[:], y_ps[:])
             nc.sync.dma_start(out_rows[:, groups[0] : groups[-1] + 1, places], y_sb[:])
 
+        warm = bank([P, I], F32, "warm", 1)
+        for n in range(3):
+            project(ROWS[0], warm[:])
         add(1, 0, 0)
         add(0, 0, 0)
         add(1, 1, 1)
@@ -202,11 +210,11 @@ def tile_attend_headpage_proj_kernel(tc, emb_words, emb_scales, wv, base, wo, of
         multiply([0, 1], slice(P, 2 * P), 2, nc.scalar.copy)
         weave(nc.vector.tensor_copy, 2)
         weave(nc.vector.tensor_copy, 3)
-        multiply([2, 3], slice(0, P), 6, nc.scalar.copy)
+        multiply([2, 3], slice(0, P), 3, nc.scalar.copy)
         multiply([2, 3], slice(P, 2 * P), 7, nc.scalar.copy)
         quantise_x(2)
         quantise_x(3)
-        multiply([0, 1], slice(2 * P, 3 * P), 3, nc.vector.tensor_copy)
+        multiply([0, 1], slice(2 * P, 3 * P), 6, nc.vector.tensor_copy)
         multiply([2, 3], slice(2 * P, 3 * P), 5, nc.scalar.copy)
         multiply([0, 1], slice(3 * P, T), 0, nc.vector.tensor_copy)
         multiply([2, 3], slice(3 * P, T), 1, nc.scalar.copy)

@@ -210,11 +210,9 @@ def tile_attend_headpage_proj_kernel(tc, emb_words, emb_scales, wv, base, wo, of
         multiply([0, 1], slice(P, 2 * P), 2, nc.scalar.copy)
         weave(nc.vector.tensor_copy, 2)
         weave(nc.vector.tensor_copy, 3)
-        multiply([2, 3], slice(0, P), 3, nc.scalar.copy)
-        multiply([2, 3], slice(P, 2 * P), 7, nc.scalar.copy)
+        multiply([2], slice(0, 2 * P), 3, nc.scalar.copy)
+        multiply([3], slice(0, 2 * P), 7, nc.scalar.copy)
         quantise_x(2)
         quantise_x(3)
-        multiply([0, 1], slice(2 * P, 3 * P), 6, nc.vector.tensor_copy)
-        multiply([2, 3], slice(2 * P, 3 * P), 5, nc.scalar.copy)
-        multiply([0, 1], slice(3 * P, T), 0, nc.vector.tensor_copy)
-        multiply([2, 3], slice(3 * P, T), 1, nc.scalar.copy)
+        for g, (b, copy) in enumerate([(6, nc.vector.tensor_copy), (5, nc.scalar.copy), (0, nc.vector.tensor_copy), (1, nc.scalar.copy)]):
+            multiply([g], slice(2 * P, T), b, copy)

@@ -20,6 +20,7 @@ P = 128
 PACK = 4
 LIST_ROWS = 16
 QUADRANT = 32
+QUADRANT_SCALES = 4
 SCALE_ROWS = K // 32
 SCALE_AT = P - SCALE_ROWS
 M_VECTOR = (32, 84)
@@ -60,19 +61,16 @@ def tile_attend_headpage_proj_kernel(tc, emb_words, emb_scales, wv, base, wo, of
         nc.sync.dma_start(wv_raw[1][:], wv_rows[:, 2:, :])
         nc.sync.dma_start(words[:].bitcast(I32), emb_words[0].bitcast(I32))
         nc.sync.dma_start(offs2_sb[:], offs2)
-        base_rows = base.rearrange("(p j) t -> p j t", j=PACK)
         got_rows = sbuf([P, I], U8, "got_rows")
         nc.vector.tensor_copy(got_rows[:], scales[:].indirect(offs_sb[:]))
-        for q in range(4):
-            nc.sync.dma_start(got_scales[QUADRANT * q : QUADRANT * q + 4, :].bitcast(I32),
-                              got_rows[SCALE_AT + 4 * q : SCALE_AT + 4 * q + 4, :].bitcast(I32))
+        for q in range(P // QUADRANT):
+            row = SCALE_AT + QUADRANT_SCALES * q
+            nc.sync.dma_start(got_scales[QUADRANT * q : QUADRANT * q + QUADRANT_SCALES, :].bitcast(I32),
+                              got_rows[row : row + QUADRANT_SCALES, :].bitcast(I32))
         wo_raw = sbuf([P, PACK, F], F32, "wo_raw", tag="scales")
         nc.sync.dma_start(wo_raw[:], wo.rearrange("(p j) f -> p j f", j=PACK))
         for j in range(PACK):
             nc.vector.memset(page[j][:], 0.0)
-
-        def base_row(j):
-            return base_sb[j // 2][:, j % 2, :]
 
         wv_bf = sbuf([P, PACK, P, PACK], BF16, "wv_bf")
         for h in range(2):
@@ -81,19 +79,23 @@ def tile_attend_headpage_proj_kernel(tc, emb_words, emb_scales, wv, base, wo, of
             nc.scalar.copy(dst[:, M_VECTOR[h] :], src[:, M_VECTOR[h] :])
             nc.vector.tensor_copy(dst[:, : M_VECTOR[h]], src[:, : M_VECTOR[h]])
 
+        base_rows = base.rearrange("(p j) t -> p j t", j=PACK)
         base_sb = {}
         for h, u in enumerate((1, 0)):
             base_sb[u] = sbuf([P, 2, T], F32, "base_sb%d" % u, tag="wv_raw%d" % h)
             nc.sync.dma_start(base_sb[u][:], base_rows[:, 2 * u : 2 * u + 2, :])
+
+        def base_row(j):
+            return base_sb[j // 2][:, j % 2, :]
 
         wv_codes = sbuf([P, E], U32, "wv_codes")
         first_scales = sbuf([P, P], U8, "first_scales")
         got_words = sbuf([P, I], U16, "got_words")
         wv_scales = {}
 
-        def quantise_wv(j, plane):
-            wv_scales[j] = plane
-            nc.vector.quantize_mx(out=wv_codes[:, j * P : (j + 1) * P].bitcast(FP8X4), scales=plane,
+        def quantise_wv(j, scale_tile):
+            wv_scales[j] = scale_tile
+            nc.vector.quantize_mx(out=wv_codes[:, j * P : (j + 1) * P].bitcast(FP8X4), scales=scale_tile,
                                   in_=wv_bf[:, j].rearrange("p m r -> p (m r)"))
 
         quantise_wv(ROWS[0], first_scales[:])
@@ -102,21 +104,21 @@ def tile_attend_headpage_proj_kernel(tc, emb_words, emb_scales, wv, base, wo, of
         for at, j in enumerate(ROWS[1:]):
             quantise_wv(j, later_scales[:, at * P : (at + 1) * P])
 
-
-        def project(j, v_ps, slots=slice(0, I)):
+        def project(j, v_ps, slots):
             nc.tensor.matmul_mx(out=v_ps, lhsT=wv_codes[:, j * P : (j + 1) * P].bitcast(FP8X4), lhsT_scale=wv_scales[j],
                                 rhs=got_words[:, slots].bitcast(FP4X4), rhs_scale=got_scales[:, slots], start=True, stop=True)
 
         v_sb = sbuf([P, PACK, I], F32, "v_sb")
-        pieces = [(0, slice(0, I // 2)), (1, slice(0, I)), (0, slice(I // 2, I))]
-        for b, (at, slots) in zip((0, 1, 7), pieces):
+        all_slots = slice(0, I)
+        first_pieces = [(0, slice(0, I // 2)), (1, all_slots), (0, slice(I // 2, I))]
+        for b, (at, slots) in zip((0, 1, 7), first_pieces):
             v_ps = bank([P, slots.stop - slots.start], F32, "v_ps%d" % b, b)
             project(ROWS[at], v_ps[:], slots)
             nc.scalar.copy(v_sb[:, at, slots], v_ps[:])
-        v_ps = bank([P, 2, I], F32, "v_ps2", 2)
+        v_late = bank([P, 2, I], F32, "v_late", 2)
         for at in range(2, PACK):
-            project(ROWS[at], v_ps[:, at - 2])
-        nc.scalar.copy(v_sb[:, 2:], v_ps[:])
+            project(ROWS[at], v_late[:, at - 2], all_slots)
+        nc.scalar.copy(v_sb[:, 2:], v_late[:])
 
         wo_bf = [sbuf([P, F // 2, PACK], BF16, "wo_bf%d" % h) for h in range(2)]
         for h in range(2):
@@ -124,16 +126,18 @@ def tile_attend_headpage_proj_kernel(tc, emb_words, emb_scales, wv, base, wo, of
                            wo_raw[:, :, h * F // 2 : (h + 1) * F // 2].rearrange("p j (c i) -> p c j i", i=4))
         wo_codes = sbuf([P, F], U32, "wo_codes")
 
-        for at, slots in pieces + [(2, slice(0, I)), (3, slice(0, I))]:
-            nc.vector.tensor_copy(page[ROWS[at]][:].indirect(offs2_sb[:, slots.start // LIST_ROWS : slots.stop // LIST_ROWS]), v_sb[:, at, slots])
+        for at, slots in first_pieces + [(2, all_slots), (3, all_slots)]:
+            entries = offs2_sb[:, slots.start // LIST_ROWS : slots.stop // LIST_ROWS]
+            nc.vector.tensor_copy(page[ROWS[at]][:].indirect(entries), v_sb[:, at, slots])
 
         x_bf = sbuf([P, T, PACK], BF16, "x_bf")
         x_words = x_bf[:].rearrange("p t j -> p (t j)").bitcast(F32).rearrange("p (t u) -> p t u", u=2)
         sums = [bank([P, 2, 2, P], F32, "sums%d" % h, 3 + h) for h in range(2)]
-        for at, row in enumerate([base_row(2), base_row(3), page[2], page[3]]):
+        terms = [(2, base_row(2)), (3, base_row(3)), (3, page[3]), (2, page[2])]
+        for at, (j, term) in enumerate(terms):
             for c in range(CHUNKS):
-                nc.tensor.matmul(sums[c // 2][:, c % 2, at % 2, :], lhsT=row[:, c * P : (c + 1) * P], rhs=ident_f32[:], is_transpose=True,
-                                 start=at == 0 and c % 2 == 0, stop=at == 3 and c % 2 == 1)
+                nc.tensor.matmul(sums[c // 2][:, c % 2, j % 2, :], lhsT=term[:, c * P : (c + 1) * P], rhs=ident_f32[:], is_transpose=True,
+                                 start=at == 0 and c % 2 == 0, stop=at == len(terms) - 1 and c % 2 == 1)
         pairs = [sbuf([P, 2, P, 2], BF16, "pairs%d" % h) for h in range(2)]
         for h in range(2):
             nc.scalar.copy(pairs[h][:], sums[h][:].rearrange("t n e p -> t n p e"))
@@ -146,73 +150,79 @@ def tile_attend_headpage_proj_kernel(tc, emb_words, emb_scales, wv, base, wo, of
 
         lay_pairs(0)
         third = bank([P, 2, P], F32, "third", 6)
-        for at, row in enumerate([base_row(1), page[1]]):
+        for at, term in enumerate([base_row(1), page[1]]):
             for n in range(2):
-                nc.tensor.matmul(third[:, n, :], lhsT=row[:, (2 + n) * P : (3 + n) * P], rhs=ident_f32[:], is_transpose=True,
+                nc.tensor.matmul(third[:, n, :], lhsT=term[:, (2 + n) * P : (3 + n) * P], rhs=ident_f32[:], is_transpose=True,
                                  start=at == 0 and n == 0, stop=at == 1 and n == 1)
         third_bf = sbuf([P, 2, P], BF16, "third_bf")
         nc.scalar.copy(third_bf[:], third[:])
         lay_pairs(1)
 
-        x_rows = sbuf([P, 2, T], BF16, "x_rows", tag="pairs1")
+        x_rows = sbuf([P, CHUNKS, 2, P], BF16, "x_rows", tag="pairs1")
         third_back = bank([P, 2 * P], BF16, "third_back", 5)
         for n in range(2):
             nc.tensor.transpose(third_back[:, n * P : (n + 1) * P], third_bf[:, n], ident_bf[:])
-        nc.scalar.copy(x_rows[:, 1, 2 * P :], third_back[:])
+        nc.scalar.copy(x_rows[:, 2:, 1, :], third_back[:].rearrange("p (c t) -> p c t", t=P))
         wo_scales = sbuf([P, F], U8, "wo_scales", tag="ident_f32")
 
-        def quantise_wo(first, last):
-            cols = slice(first * P, (last + 1) * P)
+        def quantise_wo(h):
+            cols = slice(h * F // 2, (h + 1) * F // 2)
             nc.vector.quantize_mx(out=wo_codes[:, cols].bitcast(FP8X4), scales=wo_scales[:, cols],
-                                  in_=wo_bf[first // 2][:, first % 2 * P : (last % 2 + 1) * P].rearrange("p f j -> p (f j)"))
+                                  in_=wo_bf[h][:].rearrange("p f j -> p (f j)"))
+
+        def chunks(first, last):
+            return slice(first * P, (last + 1) * P)
 
         def add(j, first, last):
-            places = slice(first * P, (last + 1) * P)
-            nc.vector.tensor_tensor(x_rows[:, j, places], page[j][:, places], base_row(j)[:, places], ADD)
+            places = chunks(first, last)
+            nc.vector.tensor_tensor(x_rows[:, first : last + 1, j, :], page[j][:, places].rearrange("p (c t) -> p c t", t=P),
+                                    base_row(j)[:, places].rearrange("p (c t) -> p c t", t=P), ADD)
 
         def weave(copy, c):
-            copy(x_bf[:, c * P : (c + 1) * P, :2], x_rows[:, :, c * P : (c + 1) * P].rearrange("p j t -> p t j"))
+            copy(x_bf[:, chunks(c, c), :2], x_rows[:, c].rearrange("p j t -> p t j"))
 
         x_codes = sbuf([P, T], U32, "x_codes")
         x_scales = sbuf([P, T], U8, "x_scales")
         out_rows = out.rearrange("(g p) t -> p g t", p=P)
 
         def quantise_x(c):
-            nc.vector.quantize_mx(out=x_codes[:, c * P : (c + 1) * P].bitcast(FP8X4), scales=x_scales[:, c * P : (c + 1) * P],
-                                  in_=x_bf[:, c * P : (c + 1) * P].rearrange("p t j -> p (t j)"))
+            nc.vector.quantize_mx(out=x_codes[:, chunks(c, c)].bitcast(FP8X4), scales=x_scales[:, chunks(c, c)],
+                                  in_=x_bf[:, chunks(c, c)].rearrange("p t j -> p (t j)"))
 
-        def multiply(groups, places, b, copy):
+        def multiply(groups, spans, b, copy):
+            places = slice(spans[0].start, spans[-1].stop)
             width = places.stop - places.start
             y_ps = bank([P, len(groups), width], F32, "y_ps%d_%d" % (groups[0], places.start), b)
             for n, g in enumerate(groups):
-                nc.tensor.matmul_mx(out=y_ps[:, n, :], lhsT=wo_codes[:, g * P : (g + 1) * P].bitcast(FP8X4),
-                                    lhsT_scale=wo_scales[:, g * P : (g + 1) * P],
-                                    rhs=x_codes[:, places].bitcast(FP8X4), rhs_scale=x_scales[:, places], start=True, stop=True)
+                for span in spans:
+                    nc.tensor.matmul_mx(out=y_ps[:, n, span.start - places.start : span.stop - places.start],
+                                        lhsT=wo_codes[:, g * P : (g + 1) * P].bitcast(FP8X4), lhsT_scale=wo_scales[:, g * P : (g + 1) * P],
+                                        rhs=x_codes[:, span].bitcast(FP8X4), rhs_scale=x_scales[:, span], start=True, stop=True)
             y_sb = sbuf([P, len(groups), width], F32, "y_sb%d_%d" % (groups[0], places.start))
             copy(y_sb[:], y_ps[:])
             nc.sync.dma_start(out_rows[:, groups[0] : groups[-1] + 1, places], y_sb[:])
 
-        warm = bank([P, I], F32, "warm", 1)
-        for n in range(3):
-            project(ROWS[0], warm[:])
         add(1, 0, 0)
         add(0, 0, 0)
         add(1, 1, 1)
-        weave(nc.vector.tensor_copy, 0)
         add(0, 1, 1)
+        weave(nc.vector.tensor_copy, 0)
         weave(nc.scalar.copy, 1)
-        quantise_wo(0, 1)
+        quantise_wo(0)
         quantise_x(0)
-        add(0, 2, 3)
         quantise_x(1)
-        multiply([0, 1], slice(0, P), 4, nc.scalar.copy)
-        quantise_wo(2, 3)
-        multiply([0, 1], slice(P, 2 * P), 2, nc.scalar.copy)
+        add(0, 2, 3)
+        multiply([0], [chunks(0, 0)], 4, nc.scalar.copy)
+        multiply([1], [chunks(0, 0)], 0, nc.scalar.copy)
+        quantise_wo(1)
+        multiply([0, 1], [chunks(1, 1)], 2, nc.scalar.copy)
         weave(nc.vector.tensor_copy, 2)
         weave(nc.vector.tensor_copy, 3)
-        multiply([2], slice(0, 2 * P), 3, nc.scalar.copy)
-        multiply([3], slice(0, 2 * P), 7, nc.scalar.copy)
+        multiply([2], [chunks(0, 1)], 3, nc.scalar.copy)
+        multiply([3], [chunks(0, 1)], 7, nc.scalar.copy)
         quantise_x(2)
         quantise_x(3)
-        for g, (b, copy) in enumerate([(6, nc.vector.tensor_copy), (5, nc.scalar.copy), (0, nc.vector.tensor_copy), (1, nc.scalar.copy)]):
-            multiply([g], slice(2 * P, T), b, copy)
+        multiply([0], [chunks(2, 2), chunks(3, 3)], 6, nc.vector.tensor_copy)
+        multiply([1], [chunks(2, 3)], 5, nc.scalar.copy)
+        multiply([2], [chunks(2, 3)], 1, nc.vector.tensor_copy)
+        multiply([3], [chunks(2, 3)], 4, nc.scalar.copy)

@@ -32,6 +32,7 @@ def tile_attend_headpage_proj_kernel(tc, emb_words, emb_scales, wv, base, wo, of
     nc = tc.nc
     with ExitStack() as ctx:
         keep = ctx.enter_context(tc.tile_pool(name="keep", bufs=1))
+        shared = ctx.enter_context(tc.tile_pool(name="shared", bufs=1))
         psum = ctx.enter_context(tc.psum_pool(name="psum", bufs=1))
 
         def sbuf(shape, dtype, name, tag=None):
@@ -43,9 +44,9 @@ def tile_attend_headpage_proj_kernel(tc, emb_words, emb_scales, wv, base, wo, of
         offs_sb = keep.tile([P, I // LIST_ROWS], U16, name="offs_sb")
         offs2_sb = keep.tile([P, I // LIST_ROWS], U16, name="offs2_sb")
         words = sbuf([P, U], U16, "words")
-        scales = sbuf([P, U], U8, "scales")
+        scales = shared.tile([P, U], U8, name="scales", offset=U // 2)
         wv_raw = [sbuf([P, 2, E], F32, "wv_raw%d" % h) for h in range(2)]
-        page = [sbuf([P, T], F32, "page%d" % j) for j in range(PACK)]
+        page = {j: sbuf([P, T], F32, "page%d" % j) for j in ROWS[:2]}
         ident_f32 = sbuf([P, P], F32, "ident_f32")
         ident_bf = sbuf([P, P], BF16, "ident_bf")
 
@@ -53,7 +54,7 @@ def tile_attend_headpage_proj_kernel(tc, emb_words, emb_scales, wv, base, wo, of
         got_scales = sbuf([P, I], U8, "got_scales")
         nc.vector.memset(got_scales[:].bitcast(I32), 0)
         make_identity(nc, ident_f32[:])
-        make_identity(nc, ident_bf[:])
+        nc.scalar.copy(ident_bf[:], ident_f32[:])
         wv_rows = wv.rearrange("(p r) e -> p r e", r=PACK)
         nc.sync.dma_start(scales[SCALE_AT:, :].bitcast(I32), emb_scales[0].bitcast(I32))
         nc.sync.dma_start(offs_sb[:], offs)
@@ -67,9 +68,11 @@ def tile_attend_headpage_proj_kernel(tc, emb_words, emb_scales, wv, base, wo, of
             row = SCALE_AT + QUADRANT_SCALES * q
             nc.sync.dma_start(got_scales[QUADRANT * q : QUADRANT * q + QUADRANT_SCALES, :].bitcast(I32),
                               got_rows[row : row + QUADRANT_SCALES, :].bitcast(I32))
-        wo_raw = sbuf([P, PACK, F], F32, "wo_raw", tag="scales")
+        page[ROWS[2]] = shared.tile([P, T], F32, name="page_third", offset=0)
+        page[ROWS[3]] = sbuf([P, T], F32, "page_last")
+        wo_raw = shared.tile([P, PACK, F], F32, name="wo_raw", offset=U)
         nc.sync.dma_start(wo_raw[:], wo.rearrange("(p j) f -> p j f", j=PACK))
-        for j in range(PACK):
+        for j in ROWS:
             nc.vector.memset(page[j][:], 0.0)
 
         wv_bf = sbuf([P, PACK, P, PACK], BF16, "wv_bf")

@@ -23,8 +23,9 @@ QUADRANT = 32
 QUADRANT_SCALES = 4
 SCALE_ROWS = K // 32
 SCALE_AT = P - SCALE_ROWS
-M_VECTOR = (32, 84)
 CHUNKS = T // P
+PAIRS_AT = 10240
+IDENT_AT = PAIRS_AT + 1024
 ROWS = (2, 3, 1, 0)
 
 
@@ -41,25 +42,26 @@ def tile_attend_headpage_proj_kernel(tc, emb_words, emb_scales, wv, base, wo, of
         def bank(shape, dtype, name, b):
             return psum.tile(shape, dtype, name=name, tag="bank%d" % b)
 
+        def placed(shape, dtype, name, offset):
+            return shared.tile(shape, dtype, name=name, offset=offset, align_bytes=64)
+
         offs_sb = keep.tile([P, I // LIST_ROWS], U16, name="offs_sb")
         offs2_sb = keep.tile([P, I // LIST_ROWS], U16, name="offs2_sb")
         words = sbuf([P, U], U16, "words")
         scales = shared.tile([P, U], U8, name="scales", offset=U // 2)
-        wv_raw = [sbuf([P, 2, E], F32, "wv_raw%d" % h) for h in range(2)]
+        wv_raw = sbuf([P, PACK, E], F32, "wv_raw")
         page = {j: sbuf([P, T], F32, "page%d" % j) for j in ROWS[:2]}
-        ident_f32 = sbuf([P, P], F32, "ident_f32")
+        ident_f32 = placed([P, P], F32, "ident_f32", IDENT_AT)
         ident_bf = sbuf([P, P], BF16, "ident_bf")
 
+        nc.scalar.dma_start(scales[SCALE_AT:, :].bitcast(I32), emb_scales[0].bitcast(I32))
         nc.vector.memset(scales[:SCALE_AT].bitcast(I32), 0)
         got_scales = sbuf([P, I], U8, "got_scales")
         nc.vector.memset(got_scales[:].bitcast(I32), 0)
         make_identity(nc, ident_f32[:])
         nc.scalar.copy(ident_bf[:], ident_f32[:])
-        wv_rows = wv.rearrange("(p r) e -> p r e", r=PACK)
-        nc.sync.dma_start(scales[SCALE_AT:, :].bitcast(I32), emb_scales[0].bitcast(I32))
         nc.sync.dma_start(offs_sb[:], offs)
-        nc.sync.dma_start(wv_raw[0][:], wv_rows[:, :2, :])
-        nc.sync.dma_start(wv_raw[1][:], wv_rows[:, 2:, :])
+        nc.sync.dma_start(wv_raw[:], wv.rearrange("(p r) e -> p r e", r=PACK))
         nc.sync.dma_start(words[:].bitcast(I32), emb_words[0].bitcast(I32))
         nc.sync.dma_start(offs2_sb[:], offs2)
         got_rows = sbuf([P, I], U8, "got_rows")
@@ -75,21 +77,21 @@ def tile_attend_headpage_proj_kernel(tc, emb_words, emb_scales, wv, base, wo, of
         for j in ROWS:
             nc.vector.memset(page[j][:], 0.0)
 
-        wv_bf = sbuf([P, PACK, P, PACK], BF16, "wv_bf")
-        for h in range(2):
-            src = wv_raw[h][:].rearrange("p r (m j) -> p m j r", j=PACK)
-            dst = wv_bf[:, :, :, 2 * h : 2 * h + 2].rearrange("p j m r -> p m j r")
-            nc.scalar.copy(dst[:, M_VECTOR[h] :], src[:, M_VECTOR[h] :])
-            nc.vector.tensor_copy(dst[:, : M_VECTOR[h]], src[:, : M_VECTOR[h]])
+        wv_bf = [sbuf([P, 2, P, PACK], BF16, "wv_bf%d" % u) for u in range(2)]
+        wv_cols = wv_raw[:].rearrange("p r (m j) -> p m r j", j=PACK)
+        for u, copy in ((1, nc.vector.tensor_copy), (0, nc.scalar.copy)):
+            copy(wv_bf[u][:].rearrange("p i m r -> p m r i"), wv_cols[:, :, :, 2 * u : 2 * u + 2])
 
         base_rows = base.rearrange("(p j) t -> p j t", j=PACK)
         base_sb = {}
-        for h, u in enumerate((1, 0)):
-            base_sb[u] = sbuf([P, 2, T], F32, "base_sb%d" % u, tag="wv_raw%d" % h)
-            nc.sync.dma_start(base_sb[u][:], base_rows[:, 2 * u : 2 * u + 2, :])
+        for first, last, tag in ((3, 3, "got_rows"), (2, 2, "wv_raw"), (0, 1, "wv_bf1")):
+            rows = sbuf([P, last + 1 - first, T], F32, "base_sb%d" % first, tag=tag)
+            nc.sync.dma_start(rows[:], base_rows[:, first : last + 1, :])
+            for j in range(first, last + 1):
+                base_sb[j] = rows[:, j - first, :]
 
         def base_row(j):
-            return base_sb[j // 2][:, j % 2, :]
+            return base_sb[j]
 
         wv_codes = sbuf([P, E], U32, "wv_codes")
         first_scales = sbuf([P, P], U8, "first_scales")
@@ -99,7 +101,7 @@ def tile_attend_headpage_proj_kernel(tc, emb_words, emb_scales, wv, base, wo, of
         def quantise_wv(j, scale_tile):
             wv_scales[j] = scale_tile
             nc.vector.quantize_mx(out=wv_codes[:, j * P : (j + 1) * P].bitcast(FP8X4), scales=scale_tile,
-                                  in_=wv_bf[:, j].rearrange("p m r -> p (m r)"))
+                                  in_=wv_bf[j // 2][:, j % 2].rearrange("p m r -> p (m r)"))
 
         quantise_wv(ROWS[0], first_scales[:])
         nc.vector.tensor_copy(got_words[:], words[:].indirect(offs_sb[:]))
@@ -136,12 +138,12 @@ def tile_attend_headpage_proj_kernel(tc, emb_words, emb_scales, wv, base, wo, of
         x_bf = sbuf([P, T, PACK], BF16, "x_bf")
         x_words = x_bf[:].rearrange("p t j -> p (t j)").bitcast(F32).rearrange("p (t u) -> p t u", u=2)
         sums = [bank([P, 2, 2, P], F32, "sums%d" % h, 3 + h) for h in range(2)]
-        terms = [(2, base_row(2)), (3, base_row(3)), (3, page[3]), (2, page[2])]
+        terms = [(3, base_row(3)), (2, base_row(2)), (3, page[3]), (2, page[2])]
         for at, (j, term) in enumerate(terms):
             for c in range(CHUNKS):
                 nc.tensor.matmul(sums[c // 2][:, c % 2, j % 2, :], lhsT=term[:, c * P : (c + 1) * P], rhs=ident_f32[:], is_transpose=True,
                                  start=at == 0 and c % 2 == 0, stop=at == len(terms) - 1 and c % 2 == 1)
-        pairs = [sbuf([P, 2, P, 2], BF16, "pairs%d" % h) for h in range(2)]
+        pairs = [sbuf([P, 2, P, 2], BF16, "pairs0"), placed([P, 2, P, 2], BF16, "pairs1", PAIRS_AT)]
         for h in range(2):
             nc.scalar.copy(pairs[h][:], sums[h][:].rearrange("t n e p -> t n p e"))
 
@@ -152,37 +154,42 @@ def tile_attend_headpage_proj_kernel(tc, emb_words, emb_scales, wv, base, wo, of
             nc.scalar.copy(x_words[:, h * 2 * P : (h + 1) * 2 * P, :], held[:].unsqueeze(2).to_broadcast([P, 2 * P, 2]))
 
         lay_pairs(0)
-        third = bank([P, 2, P], F32, "third", 6)
+        TURNED = 2
+        third = bank([P, TURNED, P], F32, "third", 6)
         for at, term in enumerate([base_row(1), page[1]]):
-            for n in range(2):
+            for n in range(TURNED):
                 nc.tensor.matmul(third[:, n, :], lhsT=term[:, (2 + n) * P : (3 + n) * P], rhs=ident_f32[:], is_transpose=True,
-                                 start=at == 0 and n == 0, stop=at == 1 and n == 1)
-        third_bf = sbuf([P, 2, P], BF16, "third_bf")
+                                 start=at == 0 and n == 0, stop=at == 1 and n == TURNED - 1)
+        third_bf = sbuf([P, TURNED, P], BF16, "third_bf")
         nc.scalar.copy(third_bf[:], third[:])
         lay_pairs(1)
 
-        x_rows = sbuf([P, CHUNKS, 2, P], BF16, "x_rows", tag="pairs1")
-        third_back = bank([P, 2 * P], BF16, "third_back", 5)
-        for n in range(2):
+        x_first = placed([P, 2, P], BF16, "x_first", PAIRS_AT)
+        x_second = placed([P, 2, P], BF16, "x_second", PAIRS_AT + 512)
+        x_last = placed([P, 2, 2, P], BF16, "x_last", IDENT_AT + 256)
+        x_rows = [x_first[:], x_second[:], x_last[:, 0], x_last[:, 1]]
+        third_back = bank([P, TURNED * P], BF16, "third_back", 5)
+        for n in range(TURNED):
             nc.tensor.transpose(third_back[:, n * P : (n + 1) * P], third_bf[:, n], ident_bf[:])
-        nc.scalar.copy(x_rows[:, 2:, 1, :], third_back[:].rearrange("p (c t) -> p c t", t=P))
-        wo_scales = sbuf([P, F], U8, "wo_scales", tag="ident_f32")
+        nc.scalar.copy(x_last[:, :, 1, :], third_back[:].rearrange("p (c t) -> p c t", t=P))
+        wo_scales = {}
 
-        def quantise_wo(h):
-            cols = slice(h * F // 2, (h + 1) * F // 2)
-            nc.vector.quantize_mx(out=wo_codes[:, cols].bitcast(FP8X4), scales=wo_scales[:, cols],
-                                  in_=wo_bf[h][:].rearrange("p f j -> p (f j)"))
+        def quantise_wo(first, last, scale_tile):
+            cols = slice(first * P, (last + 1) * P)
+            for g in range(first, last + 1):
+                wo_scales[g] = scale_tile[:, (g - first) * P : (g - first + 1) * P]
+            h, at = first // 2, first % 2
+            nc.vector.quantize_mx(out=wo_codes[:, cols].bitcast(FP8X4), scales=scale_tile[:, : (last + 1 - first) * P],
+                                  in_=wo_bf[h][:, at * P : (at + last + 1 - first) * P].rearrange("p f j -> p (f j)"))
 
         def chunks(first, last):
             return slice(first * P, (last + 1) * P)
 
-        def add(j, first, last):
-            places = chunks(first, last)
-            nc.vector.tensor_tensor(x_rows[:, first : last + 1, j, :], page[j][:, places].rearrange("p (c t) -> p c t", t=P),
-                                    base_row(j)[:, places].rearrange("p (c t) -> p c t", t=P), ADD)
+        def add(j, c):
+            nc.vector.tensor_tensor(x_rows[c][:, j, :], page[j][:, chunks(c, c)], base_row(j)[:, chunks(c, c)], ADD)
 
         def weave(copy, c):
-            copy(x_bf[:, chunks(c, c), :2], x_rows[:, c].rearrange("p j t -> p t j"))
+            copy(x_bf[:, chunks(c, c), :2], x_rows[c].rearrange("p j t -> p t j"))
 
         x_codes = sbuf([P, T], U32, "x_codes")
         x_scales = sbuf([P, T], U8, "x_scales")
@@ -192,40 +199,50 @@ def tile_attend_headpage_proj_kernel(tc, emb_words, emb_scales, wv, base, wo, of
             nc.vector.quantize_mx(out=x_codes[:, chunks(c, c)].bitcast(FP8X4), scales=x_scales[:, chunks(c, c)],
                                   in_=x_bf[:, chunks(c, c)].rearrange("p t j -> p (t j)"))
 
-        def multiply(groups, spans, b, copy):
+        def multiply(groups, spans, b, copy, y_sb):
             places = slice(spans[0].start, spans[-1].stop)
             width = places.stop - places.start
             y_ps = bank([P, len(groups), width], F32, "y_ps%d_%d" % (groups[0], places.start), b)
             for n, g in enumerate(groups):
                 for span in spans:
                     nc.tensor.matmul_mx(out=y_ps[:, n, span.start - places.start : span.stop - places.start],
-                                        lhsT=wo_codes[:, g * P : (g + 1) * P].bitcast(FP8X4), lhsT_scale=wo_scales[:, g * P : (g + 1) * P],
+                                        lhsT=wo_codes[:, g * P : (g + 1) * P].bitcast(FP8X4), lhsT_scale=wo_scales[g],
                                         rhs=x_codes[:, span].bitcast(FP8X4), rhs_scale=x_scales[:, span], start=True, stop=True)
-            y_sb = sbuf([P, len(groups), width], F32, "y_sb%d_%d" % (groups[0], places.start))
-            copy(y_sb[:], y_ps[:])
+            copy(y_sb, y_ps[:])
+
+        def put_out(groups, spans, b, copy):
+            places = slice(spans[0].start, spans[-1].stop)
+            y_sb = sbuf([P, len(groups), places.stop - places.start], F32, "y_sb%d_%d" % (groups[0], places.start))
+            multiply(groups, spans, b, copy, y_sb[:])
             nc.sync.dma_start(out_rows[:, groups[0] : groups[-1] + 1, places], y_sb[:])
 
-        add(1, 0, 0)
-        add(0, 0, 0)
-        add(1, 1, 1)
-        add(0, 1, 1)
+        early_scales = placed([P, 2 * P], U8, "early_scales", IDENT_AT)
+        add(1, 0)
+        add(0, 0)
+        add(1, 1)
+        add(0, 1)
         weave(nc.vector.tensor_copy, 0)
+        quantise_wo(0, 0, early_scales[:, :P])
         weave(nc.scalar.copy, 1)
-        quantise_wo(0)
+        add(0, 2)
+        weave(nc.scalar.copy, 2)
         quantise_x(0)
+        quantise_wo(1, 1, early_scales[:, P:])
         quantise_x(1)
-        add(0, 2, 3)
-        multiply([0], [chunks(0, 0)], 4, nc.scalar.copy)
-        multiply([1], [chunks(0, 0)], 0, nc.scalar.copy)
-        quantise_wo(1)
-        multiply([0, 1], [chunks(1, 1)], 2, nc.scalar.copy)
-        weave(nc.vector.tensor_copy, 2)
+        add(0, 3)
+        put_out([0], [chunks(0, 0)], 4, nc.scalar.copy)
+        put_out([1], [chunks(0, 0)], 7, nc.scalar.copy)
+        late_scales = placed([P, 2 * P], U8, "late_scales", PAIRS_AT + 512)
+        quantise_wo(2, 3, late_scales[:])
+        put_out([0, 1], [chunks(1, 1)], 2, nc.scalar.copy)
         weave(nc.vector.tensor_copy, 3)
-        multiply([2], [chunks(0, 1)], 3, nc.scalar.copy)
-        multiply([3], [chunks(0, 1)], 7, nc.scalar.copy)
+        put_out([2], [chunks(0, 1)], 3, nc.scalar.copy)
+        y_whole = sbuf([P, 1, T], F32, "y_whole")
+        multiply([3], [chunks(0, 1)], 0, nc.scalar.copy, y_whole[:, :, chunks(0, 1)])
         quantise_x(2)
         quantise_x(3)
-        multiply([0], [chunks(2, 2), chunks(3, 3)], 6, nc.vector.tensor_copy)
-        multiply([1], [chunks(2, 3)], 5, nc.scalar.copy)
-        multiply([2], [chunks(2, 3)], 1, nc.vector.tensor_copy)
-        multiply([3], [chunks(2, 3)], 4, nc.scalar.copy)
+        put_out([0], [chunks(2, 2), chunks(3, 3)], 6, nc.vector.tensor_copy)
+        put_out([1], [chunks(2, 3)], 5, nc.scalar.copy)
+        put_out([2], [chunks(2, 3)], 1, nc.vector.tensor_copy)
+        multiply([3], [chunks(2, 3)], 4, nc.scalar.copy, y_whole[:, :, chunks(2, 3)])
+        nc.scalar.dma_start(out_rows[:, 3:, :], y_whole[:])

@@ -237,12 +237,10 @@ def tile_attend_headpage_proj_kernel(tc, emb_words, emb_scales, wv, base, wo, of
         put_out([0, 1], [chunks(1, 1)], 2, nc.scalar.copy)
         weave(nc.vector.tensor_copy, 3)
         put_out([2], [chunks(0, 1)], 3, nc.scalar.copy)
-        y_whole = sbuf([P, 1, T], F32, "y_whole")
-        multiply([3], [chunks(0, 1)], 0, nc.scalar.copy, y_whole[:, :, chunks(0, 1)])
+        put_out([3], [chunks(0, 1)], 0, nc.scalar.copy)
         quantise_x(2)
         quantise_x(3)
         put_out([0], [chunks(2, 2), chunks(3, 3)], 6, nc.vector.tensor_copy)
         put_out([1], [chunks(2, 3)], 5, nc.scalar.copy)
         put_out([2], [chunks(2, 3)], 1, nc.vector.tensor_copy)
-        multiply([3], [chunks(2, 3)], 4, nc.scalar.copy, y_whole[:, :, chunks(2, 3)])
-        nc.scalar.dma_start(out_rows[:, 3:, :], y_whole[:])
+        put_out([3], [chunks(2, 3)], 4, nc.scalar.copy)

@@ -137,41 +137,43 @@ def tile_attend_headpage_proj_kernel(tc, emb_words, emb_scales, wv, base, wo, of
 
         x_bf = sbuf([P, T, PACK], BF16, "x_bf")
         x_words = x_bf[:].rearrange("p t j -> p (t j)").bitcast(F32).rearrange("p (t u) -> p t u", u=2)
-        sums = [bank([P, 2, 2, P], F32, "sums%d" % h, 3 + h) for h in range(2)]
+        sums = [bank([P, 2, P], F32, "sums%d" % c, 3 + c) for c in range(CHUNKS)]
         terms = [(3, base_row(3)), (2, base_row(2)), (3, page[3]), (2, page[2])]
         for at, (j, term) in enumerate(terms):
             for c in range(CHUNKS):
-                nc.tensor.matmul(sums[c // 2][:, c % 2, j % 2, :], lhsT=term[:, c * P : (c + 1) * P], rhs=ident_f32[:], is_transpose=True,
-                                 start=at == 0 and c % 2 == 0, stop=at == len(terms) - 1 and c % 2 == 1)
-        pairs = [sbuf([P, 2, P, 2], BF16, "pairs0"), placed([P, 2, P, 2], BF16, "pairs1", PAIRS_AT)]
-        for h in range(2):
-            nc.scalar.copy(pairs[h][:], sums[h][:].rearrange("t n e p -> t n p e"))
+                nc.tensor.matmul(sums[c][:, j % 2, :], lhsT=term[:, c * P : (c + 1) * P], rhs=ident_f32[:], is_transpose=True,
+                                 start=at == 0, stop=at == len(terms) - 1)
+        pairs = [placed([P, 2, P, 2], BF16, "pairs0", PAIRS_AT), sbuf([P, 2, P, 2], BF16, "pairs1")]
+        for c in range(CHUNKS):
+            nc.scalar.copy(pairs[c // 2][:, c % 2], sums[c][:].rearrange("t e p -> t p e"))
 
-        def lay_pairs(h):
+        def lay_pairs(h, pieces):
             held = bank([P, 2 * P], F32, "held%d" % h, h)
             for n in range(2):
                 nc.tensor.transpose(held[:, n * P : (n + 1) * P], pairs[h][:, n].rearrange("t p e -> t (p e)").bitcast(F32), ident_f32[:])
-            nc.scalar.copy(x_words[:, h * 2 * P : (h + 1) * 2 * P, :], held[:].unsqueeze(2).to_broadcast([P, 2 * P, 2]))
+            width = 2 * P // pieces
+            for at in range(0, 2 * P, width):
+                nc.scalar.copy(x_words[:, h * 2 * P + at : h * 2 * P + at + width, :], held[:, at : at + width].unsqueeze(2).to_broadcast([P, width, 2]))
 
-        lay_pairs(0)
+        lay_pairs(0, 2)
         TURNED = 2
-        third = bank([P, TURNED, P], F32, "third", 6)
+        third = bank([P, TURNED, P], F32, "third", 3)
         for at, term in enumerate([base_row(1), page[1]]):
             for n in range(TURNED):
                 nc.tensor.matmul(third[:, n, :], lhsT=term[:, (2 + n) * P : (3 + n) * P], rhs=ident_f32[:], is_transpose=True,
                                  start=at == 0 and n == 0, stop=at == 1 and n == TURNED - 1)
         third_bf = sbuf([P, TURNED, P], BF16, "third_bf")
         nc.scalar.copy(third_bf[:], third[:])
-        lay_pairs(1)
+        lay_pairs(1, 1)
 
         x_first = placed([P, 2, P], BF16, "x_first", PAIRS_AT)
         x_second = placed([P, 2, P], BF16, "x_second", PAIRS_AT + 512)
-        x_last = placed([P, 2, 2, P], BF16, "x_last", IDENT_AT + 256)
-        x_rows = [x_first[:], x_second[:], x_last[:, 0], x_last[:, 1]]
-        third_back = bank([P, TURNED * P], BF16, "third_back", 5)
+        x_third = placed([P, 2, P], BF16, "x_third", IDENT_AT + 256)
+        x_rows = [x_first[:], x_second[:], x_third[:]]
+        third_back = bank([P, TURNED * P], BF16, "third_back", 7)
         for n in range(TURNED):
             nc.tensor.transpose(third_back[:, n * P : (n + 1) * P], third_bf[:, n], ident_bf[:])
-        nc.scalar.copy(x_last[:, :, 1, :], third_back[:].rearrange("p (c t) -> p c t", t=P))
+        nc.scalar.copy(x_third[:, 1, :], third_back[:, :P])
         wo_scales = {}
 
         def quantise_wo(first, last, scale_tile):
@@ -224,6 +226,9 @@ def tile_attend_headpage_proj_kernel(tc, emb_words, emb_scales, wv, base, wo, of
         weave(nc.vector.tensor_copy, 0)
         quantise_wo(0, 0, early_scales[:, :P])
         weave(nc.scalar.copy, 1)
+        x_fourth = placed([P, 2, P], BF16, "x_fourth", PAIRS_AT)
+        x_rows.append(x_fourth[:])
+        nc.scalar.copy(x_fourth[:, 1, :], third_back[:, P:])
         add(0, 2)
         weave(nc.scalar.copy, 2)
         quantise_x(0)
@@ -231,16 +236,16 @@ def tile_attend_headpage_proj_kernel(tc, emb_words, emb_scales, wv, base, wo, of
         quantise_x(1)
         add(0, 3)
         put_out([0], [chunks(0, 0)], 4, nc.scalar.copy)
-        put_out([1], [chunks(0, 0)], 7, nc.scalar.copy)
+        put_out([1], [chunks(0, 0)], 5, nc.scalar.copy)
         late_scales = placed([P, 2 * P], U8, "late_scales", PAIRS_AT + 512)
         quantise_wo(2, 3, late_scales[:])
-        put_out([0, 1], [chunks(1, 1)], 2, nc.scalar.copy)
+        put_out([0, 1], [chunks(1, 1)], 3, nc.scalar.copy)
         weave(nc.vector.tensor_copy, 3)
-        put_out([2], [chunks(0, 1)], 3, nc.scalar.copy)
+        put_out([2], [chunks(0, 1)], 2, nc.scalar.copy)
         put_out([3], [chunks(0, 1)], 0, nc.scalar.copy)
         quantise_x(2)
         quantise_x(3)
         put_out([0], [chunks(2, 2), chunks(3, 3)], 6, nc.vector.tensor_copy)
-        put_out([1], [chunks(2, 3)], 5, nc.scalar.copy)
+        put_out([1], [chunks(2, 3)], 7, nc.scalar.copy)
         put_out([2], [chunks(2, 3)], 1, nc.vector.tensor_copy)
         put_out([3], [chunks(2, 3)], 4, nc.scalar.copy)

@@ -24,8 +24,9 @@ QUADRANT_SCALES = 4
 SCALE_ROWS = K // 32
 SCALE_AT = P - SCALE_ROWS
 CHUNKS = T // P
-PAIRS_AT = 10240
+PAIRS_AT = 10752
 IDENT_AT = PAIRS_AT + 1024
+TERMS_AT = IDENT_AT + 1024
 ROWS = (2, 3, 1, 0)
 
 
@@ -70,9 +71,9 @@ def tile_attend_headpage_proj_kernel(tc, emb_words, emb_scales, wv, base, wo, of
             row = SCALE_AT + QUADRANT_SCALES * q
             nc.sync.dma_start(got_scales[QUADRANT * q : QUADRANT * q + QUADRANT_SCALES, :].bitcast(I32),
                               got_rows[row : row + QUADRANT_SCALES, :].bitcast(I32))
-        page[ROWS[2]] = shared.tile([P, T], F32, name="page_third", offset=0)
-        page[ROWS[3]] = sbuf([P, T], F32, "page_last")
-        wo_raw = shared.tile([P, PACK, F], F32, name="wo_raw", offset=U)
+        page[ROWS[2]] = sbuf([P, T], F32, "page_third")
+        page[ROWS[3]] = shared.tile([P, T + P], F32, name="page_last", offset=0)
+        wo_raw = shared.tile([P, PACK, F], F32, name="wo_raw", offset=4 * (T + P))
         nc.sync.dma_start(wo_raw[:], wo.rearrange("(p j) f -> p j f", j=PACK))
         for j in ROWS:
             nc.vector.memset(page[j][:], 0.0)
@@ -166,10 +167,11 @@ def tile_attend_headpage_proj_kernel(tc, emb_words, emb_scales, wv, base, wo, of
         nc.scalar.copy(third_bf[:], third[:])
         lay_pairs(1, 1)
 
-        x_first = placed([P, 2, P], BF16, "x_first", PAIRS_AT)
+        first_terms = placed([P, 2, P], F32, "first_terms", TERMS_AT)
+        nc.scalar.copy(first_terms[:, 0], base_row(0)[:, :P])
         x_second = placed([P, 2, P], BF16, "x_second", PAIRS_AT + 512)
         x_third = placed([P, 2, P], BF16, "x_third", IDENT_AT + 256)
-        x_rows = [x_first[:], x_second[:], x_third[:]]
+        x_rows = [None, x_second[:], x_third[:]]
         third_back = bank([P, TURNED * P], BF16, "third_back", 7)
         for n in range(TURNED):
             nc.tensor.transpose(third_back[:, n * P : (n + 1) * P], third_bf[:, n], ident_bf[:])
@@ -219,14 +221,15 @@ def tile_attend_headpage_proj_kernel(tc, emb_words, emb_scales, wv, base, wo, of
             nc.sync.dma_start(out_rows[:, groups[0] : groups[-1] + 1, places], y_sb[:])
 
         early_scales = placed([P, 2 * P], U8, "early_scales", IDENT_AT)
-        add(1, 0)
-        add(0, 0)
+        nc.vector.tensor_tensor(first_terms[:, 1], page[1][:, :P], base_row(1)[:, :P], ADD)
         add(1, 1)
         add(0, 1)
-        weave(nc.vector.tensor_copy, 0)
+        nc.vector.tensor_tensor(x_bf[:, :P, :2].rearrange("p (c i) j -> p c j i", i=4),
+                                page[0][:].rearrange("p (j c i) -> p c j i", c=P // 4, i=4)[:, :, ::CHUNKS],
+                                first_terms[:].rearrange("p j (c i) -> p c j i", i=4), ADD)
         quantise_wo(0, 0, early_scales[:, :P])
         weave(nc.scalar.copy, 1)
-        x_fourth = placed([P, 2, P], BF16, "x_fourth", PAIRS_AT)
+        x_fourth = placed([P, 2, P], BF16, "x_fourth", TERMS_AT)
         x_rows.append(x_fourth[:])
         nc.scalar.copy(x_fourth[:, 1, :], third_back[:, P:])
         add(0, 2)

@@ -25,8 +25,7 @@ SCALE_ROWS = K // 32
 SCALE_AT = P - SCALE_ROWS
 CHUNKS = T // P
 PAIRS_AT = 10752
-IDENT_AT = PAIRS_AT + 1024
-TERMS_AT = IDENT_AT + 1024
+IDENT_AT = PAIRS_AT + 1536
 ROWS = (2, 3, 1, 0)
 
 
@@ -167,7 +166,7 @@ def tile_attend_headpage_proj_kernel(tc, emb_words, emb_scales, wv, base, wo, of
         nc.scalar.copy(third_bf[:], third[:])
         lay_pairs(1, 1)
 
-        first_terms = placed([P, 2, P], F32, "first_terms", TERMS_AT)
+        first_terms = sbuf([P, 2, P], F32, "first_terms")
         nc.scalar.copy(first_terms[:, 0], base_row(0)[:, :P])
         x_second = placed([P, 2, P], BF16, "x_second", PAIRS_AT + 512)
         x_third = placed([P, 2, P], BF16, "x_third", IDENT_AT + 256)
@@ -227,13 +226,13 @@ def tile_attend_headpage_proj_kernel(tc, emb_words, emb_scales, wv, base, wo, of
         nc.vector.tensor_tensor(x_bf[:, :P, :2].rearrange("p (c i) j -> p c j i", i=4),
                                 page[0][:].rearrange("p (j c i) -> p c j i", c=P // 4, i=4)[:, :, ::CHUNKS],
                                 first_terms[:].rearrange("p j (c i) -> p c j i", i=4), ADD)
-        quantise_wo(0, 0, early_scales[:, :P])
         weave(nc.scalar.copy, 1)
-        x_fourth = placed([P, 2, P], BF16, "x_fourth", TERMS_AT)
+        add(0, 2)
+        quantise_wo(0, 0, early_scales[:, :P])
+        weave(nc.scalar.copy, 2)
+        x_fourth = placed([P, 2, P], BF16, "x_fourth", PAIRS_AT + 768)
         x_rows.append(x_fourth[:])
         nc.scalar.copy(x_fourth[:, 1, :], third_back[:, P:])
-        add(0, 2)
-        weave(nc.scalar.copy, 2)
         quantise_x(0)
         quantise_wo(1, 1, early_scales[:, P:])
         quantise_x(1)
@@ -241,7 +240,8 @@ def tile_attend_headpage_proj_kernel(tc, emb_words, emb_scales, wv, base, wo, of
         put_out([0], [chunks(0, 0)], 4, nc.scalar.copy)
         put_out([1], [chunks(0, 0)], 5, nc.scalar.copy)
         late_scales = placed([P, 2 * P], U8, "late_scales", PAIRS_AT + 512)
-        quantise_wo(2, 3, late_scales[:])
+        quantise_wo(2, 2, late_scales[:, :P])
+        quantise_wo(3, 3, late_scales[:, P:])
         put_out([0, 1], [chunks(1, 1)], 3, nc.scalar.copy)
         weave(nc.vector.tensor_copy, 3)
         put_out([2], [chunks(0, 1)], 2, nc.scalar.copy)
@@ -249,6 +249,6 @@ def tile_attend_headpage_proj_kernel(tc, emb_words, emb_scales, wv, base, wo, of
         quantise_x(2)
         quantise_x(3)
         put_out([0], [chunks(2, 2), chunks(3, 3)], 6, nc.vector.tensor_copy)
-        put_out([1], [chunks(2, 3)], 7, nc.scalar.copy)
+        put_out([1], [chunks(2, 2), chunks(3, 3)], 7, nc.scalar.copy)
         put_out([2], [chunks(2, 3)], 1, nc.vector.tensor_copy)
         put_out([3], [chunks(2, 3)], 4, nc.scalar.copy)

from contextlib import ExitStack

import concourse.mybir as mybir
from concourse.masks import make_identity

K, U, I, T, E, F = 512, 2048, 256, 512, 512, 512
FLOPS = 2 * K * E * I + 2 * E * F * T

F32 = mybir.dt.float32
BF16 = mybir.dt.bfloat16
I32 = mybir.dt.int32
U32 = mybir.dt.uint32
U16 = mybir.dt.uint16
U8 = mybir.dt.uint8
FP8X4 = mybir.dt.float8_e4m3fn_x4
FP4X4 = mybir.dt.float4_e2m1fn_x4
ADD = mybir.AluOpType.add

P = 128
PACK = 4
LIST_ROWS = 16
QUADRANT = 32
QUADRANT_SCALES = 4
SCALE_ROWS = K // 32
SCALE_AT = P - SCALE_ROWS
CHUNKS = T // P
PAIRS_AT = 10752
IDENT_AT = PAIRS_AT + 1536
ROWS = (2, 3, 1, 0)


def tile_attend_headpage_proj_kernel(tc, emb_words, emb_scales, wv, base, wo, offs, offs2, out):
    nc = tc.nc
    with ExitStack() as ctx:
        keep = ctx.enter_context(tc.tile_pool(name="keep", bufs=1))
        shared = ctx.enter_context(tc.tile_pool(name="shared", bufs=1))
        psum = ctx.enter_context(tc.psum_pool(name="psum", bufs=1))

        def sbuf(shape, dtype, name, tag=None):
            return keep.tile(shape, dtype, name=name, tag=tag or name, align_bytes=64)

        def bank(shape, dtype, name, b):
            return psum.tile(shape, dtype, name=name, tag="bank%d" % b)

        def placed(shape, dtype, name, offset):
            return shared.tile(shape, dtype, name=name, offset=offset, align_bytes=64)

        offs_sb = keep.tile([P, I // LIST_ROWS], U16, name="offs_sb")
        offs2_sb = keep.tile([P, I // LIST_ROWS], U16, name="offs2_sb")
        words = sbuf([P, U], U16, "words")
        scales = shared.tile([P, U], U8, name="scales", offset=U // 2)
        wv_raw = sbuf([P, PACK, E], F32, "wv_raw")
        page = {j: sbuf([P, T], F32, "page%d" % j) for j in ROWS[:2]}
        ident_f32 = placed([P, P], F32, "ident_f32", IDENT_AT)
        ident_bf = sbuf([P, P], BF16, "ident_bf")

        nc.scalar.dma_start(scales[SCALE_AT:, :].bitcast(I32), emb_scales[0].bitcast(I32))
        nc.vector.memset(scales[:SCALE_AT].bitcast(I32), 0)
        got_scales = sbuf([P, I], U8, "got_scales")
        nc.vector.memset(got_scales[:].bitcast(I32), 0)
        make_identity(nc, ident_f32[:])
        nc.scalar.copy(ident_bf[:], ident_f32[:])
        nc.sync.dma_start(offs_sb[:], offs)
        nc.sync.dma_start(wv_raw[:], wv.rearrange("(p r) e -> p r e", r=PACK))
        nc.sync.dma_start(words[:].bitcast(I32), emb_words[0].bitcast(I32))
        nc.sync.dma_start(offs2_sb[:], offs2)
        got_rows = sbuf([P, I], U8, "got_rows")
        nc.vector.tensor_copy(got_rows[:], scales[:].indirect(offs_sb[:]))
        for q in range(P // QUADRANT):
            row = SCALE_AT + QUADRANT_SCALES * q
            nc.sync.dma_start(got_scales[QUADRANT * q : QUADRANT * q + QUADRANT_SCALES, :].bitcast(I32),
                              got_rows[row : row + QUADRANT_SCALES, :].bitcast(I32))
        page[ROWS[2]] = sbuf([P, T], F32, "page_third")
        page[ROWS[3]] = shared.tile([P, T + P], F32, name="page_last", offset=0)
        wo_raw = shared.tile([P, PACK, F], F32, name="wo_raw", offset=4 * (T + P))
        nc.sync.dma_start(wo_raw[:], wo.rearrange("(p j) f -> p j f", j=PACK))
        for j in ROWS:
            nc.vector.memset(page[j][:], 0.0)

        wv_bf = [sbuf([P, 2, P, PACK], BF16, "wv_bf%d" % u) for u in range(2)]
        wv_cols = wv_raw[:].rearrange("p r (m j) -> p m r j", j=PACK)
        for u, copy in ((1, nc.vector.tensor_copy), (0, nc.scalar.copy)):
            copy(wv_bf[u][:].rearrange("p i m r -> p m r i"), wv_cols[:, :, :, 2 * u : 2 * u + 2])

        base_rows = base.rearrange("(p j) t -> p j t", j=PACK)
        base_sb = {}
        for first, last, tag in ((3, 3, "got_rows"), (2, 2, "wv_raw"), (0, 1, "wv_bf1")):
            rows = sbuf([P, last + 1 - first, T], F32, "base_sb%d" % first, tag=tag)
            nc.sync.dma_start(rows[:], base_rows[:, first : last + 1, :])
            for j in range(first, last + 1):
                base_sb[j] = rows[:, j - first, :]

        def base_row(j):
            return base_sb[j]

        wv_codes = sbuf([P, E], U32, "wv_codes")
        first_scales = sbuf([P, P], U8, "first_scales")
        got_words = sbuf([P, I], U16, "got_words")
        wv_scales = {}

        def quantise_wv(j, scale_tile):
            wv_scales[j] = scale_tile
            nc.vector.quantize_mx(out=wv_codes[:, j * P : (j + 1) * P].bitcast(FP8X4), scales=scale_tile,
                                  in_=wv_bf[j // 2][:, j % 2].rearrange("p m r -> p (m r)"))

        quantise_wv(ROWS[0], first_scales[:])
        nc.vector.tensor_copy(got_words[:], words[:].indirect(offs_sb[:]))
        later_scales = sbuf([P, E - P], U8, "later_scales", tag="words")
        for at, j in enumerate(ROWS[1:]):
            quantise_wv(j, later_scales[:, at * P : (at + 1) * P])

        def project(j, v_ps, slots):
            nc.tensor.matmul_mx(out=v_ps, lhsT=wv_codes[:, j * P : (j + 1) * P].bitcast(FP8X4), lhsT_scale=wv_scales[j],
                                rhs=got_words[:, slots].bitcast(FP4X4), rhs_scale=got_scales[:, slots], start=True, stop=True)

        v_sb = sbuf([P, PACK, I], F32, "v_sb")
        all_slots = slice(0, I)
        first_pieces = [(0, slice(0, I // 2)), (1, all_slots), (0, slice(I // 2, I))]
        for b, (at, slots) in zip((0, 1, 7), first_pieces):
            v_ps = bank([P, slots.stop - slots.start], F32, "v_ps%d" % b, b)
            project(ROWS[at], v_ps[:], slots)
            nc.scalar.copy(v_sb[:, at, slots], v_ps[:])
        v_late = bank([P, 2, I], F32, "v_late", 2)
        for at in range(2, PACK):
            project(ROWS[at], v_late[:, at - 2], all_slots)
        nc.scalar.copy(v_sb[:, 2:], v_late[:])

        wo_bf = [sbuf([P, F // 2, PACK], BF16, "wo_bf%d" % h) for h in range(2)]
        for h in range(2):
            nc.scalar.copy(wo_bf[h][:].rearrange("p (c i) j -> p c j i", i=4),
                           wo_raw[:, :, h * F // 2 : (h + 1) * F // 2].rearrange("p j (c i) -> p c j i", i=4))
        wo_codes = sbuf([P, F], U32, "wo_codes")

        for at, slots in first_pieces + [(2, all_slots), (3, all_slots)]:
            entries = offs2_sb[:, slots.start // LIST_ROWS : slots.stop // LIST_ROWS]
            nc.vector.tensor_copy(page[ROWS[at]][:].indirect(entries), v_sb[:, at, slots])

        x_bf = sbuf([P, T, PACK], BF16, "x_bf")
        x_words = x_bf[:].rearrange("p t j -> p (t j)").bitcast(F32).rearrange("p (t u) -> p t u", u=2)
        sums = [bank([P, 2, P], F32, "sums%d" % c, 3 + c) for c in range(CHUNKS)]
        terms = [(3, base_row(3)), (2, base_row(2)), (3, page[3]), (2, page[2])]
        for at, (j, term) in enumerate(terms):
            for c in range(CHUNKS):
                nc.tensor.matmul(sums[c][:, j % 2, :], lhsT=term[:, c * P : (c + 1) * P], rhs=ident_f32[:], is_transpose=True,
                                 start=at == 0, stop=at == len(terms) - 1)
        pairs = [placed([P, 2, P, 2], BF16, "pairs0", PAIRS_AT), sbuf([P, 2, P, 2], BF16, "pairs1")]
        for c in range(CHUNKS):
            nc.scalar.copy(pairs[c // 2][:, c % 2], sums[c][:].rearrange("t e p -> t p e"))

        def lay_pairs(h, pieces):
            held = bank([P, 2 * P], F32, "held%d" % h, h)
            for n in range(2):
                nc.tensor.transpose(held[:, n * P : (n + 1) * P], pairs[h][:, n].rearrange("t p e -> t (p e)").bitcast(F32), ident_f32[:])
            width = 2 * P // pieces
            for at in range(0, 2 * P, width):
                nc.scalar.copy(x_words[:, h * 2 * P + at : h * 2 * P + at + width, :], held[:, at : at + width].unsqueeze(2).to_broadcast([P, width, 2]))

        lay_pairs(0, 2)
        TURNED = 2
        third = bank([P, TURNED, P], F32, "third", 3)
        for at, term in enumerate([base_row(1), page[1]]):
            for n in range(TURNED):
                nc.tensor.matmul(third[:, n, :], lhsT=term[:, (2 + n) * P : (3 + n) * P], rhs=ident_f32[:], is_transpose=True,
                                 start=at == 0 and n == 0, stop=at == 1 and n == TURNED - 1)
        third_bf = sbuf([P, TURNED, P], BF16, "third_bf")
        nc.scalar.copy(third_bf[:], third[:])
        lay_pairs(1, 1)

        first_terms = sbuf([P, 2, P], F32, "first_terms")
        nc.scalar.copy(first_terms[:, 0], base_row(0)[:, :P])
        x_second = placed([P, 2, P], BF16, "x_second", PAIRS_AT + 512)
        x_third = placed([P, 2, P], BF16, "x_third", IDENT_AT + 256)
        x_rows = [None, x_second[:], x_third[:]]
        third_back = bank([P, TURNED * P], BF16, "third_back", 7)
        for n in range(TURNED):
            nc.tensor.transpose(third_back[:, n * P : (n + 1) * P], third_bf[:, n], ident_bf[:])
        nc.scalar.copy(x_third[:, 1, :], third_back[:, :P])
        wo_scales = {}

        def quantise_wo(first, last, scale_tile):
            cols = slice(first * P, (last + 1) * P)
            for g in range(first, last + 1):
                wo_scales[g] = scale_tile[:, (g - first) * P : (g - first + 1) * P]
            h, at = first // 2, first % 2
            nc.vector.quantize_mx(out=wo_codes[:, cols].bitcast(FP8X4), scales=scale_tile[:, : (last + 1 - first) * P],
                                  in_=wo_bf[h][:, at * P : (at + last + 1 - first) * P].rearrange("p f j -> p (f j)"))

        def chunks(first, last):
            return slice(first * P, (last + 1) * P)

        def add(j, c):
            nc.vector.tensor_tensor(x_rows[c][:, j, :], page[j][:, chunks(c, c)], base_row(j)[:, chunks(c, c)], ADD)

        def weave(copy, c):
            copy(x_bf[:, chunks(c, c), :2], x_rows[c].rearrange("p j t -> p t j"))

        x_codes = sbuf([P, T], U32, "x_codes")
        x_scales = sbuf([P, T], U8, "x_scales")
        out_rows = out.rearrange("(g p) t -> p g t", p=P)

        def quantise_x(c):
            nc.vector.quantize_mx(out=x_codes[:, chunks(c, c)].bitcast(FP8X4), scales=x_scales[:, chunks(c, c)],
                                  in_=x_bf[:, chunks(c, c)].rearrange("p t j -> p (t j)"))

        def multiply(groups, spans, b, copy, y_sb):
            places = slice(spans[0].start, spans[-1].stop)
            width = places.stop - places.start
            y_ps = bank([P, len(groups), width], F32, "y_ps%d_%d" % (groups[0], places.start), b)
            for n, g in enumerate(groups):
                for span in spans:
                    nc.tensor.matmul_mx(out=y_ps[:, n, span.start - places.start : span.stop - places.start],
                                        lhsT=wo_codes[:, g * P : (g + 1) * P].bitcast(FP8X4), lhsT_scale=wo_scales[g],
                                        rhs=x_codes[:, span].bitcast(FP8X4), rhs_scale=x_scales[:, span], start=True, stop=True)
            copy(y_sb, y_ps[:])

        def put_out(groups, spans, b, copy):
            places = slice(spans[0].start, spans[-1].stop)
            y_sb = sbuf([P, len(groups), places.stop - places.start], F32, "y_sb%d_%d" % (groups[0], places.start))
            multiply(groups, spans, b, copy, y_sb[:])
            nc.sync.dma_start(out_rows[:, groups[0] : groups[-1] + 1, places], y_sb[:])

        early_scales = placed([P, 2 * P], U8, "early_scales", IDENT_AT)
        nc.vector.tensor_tensor(first_terms[:, 1], page[1][:, :P], base_row(1)[:, :P], ADD)
        add(1, 1)
        add(0, 1)
        nc.vector.tensor_tensor(x_bf[:, :P, :2].rearrange("p (c i) j -> p c j i", i=4),
                                page[0][:].rearrange("p (j c i) -> p c j i", c=P // 4, i=4)[:, :, ::CHUNKS],
                                first_terms[:].rearrange("p j (c i) -> p c j i", i=4), ADD)
        weave(nc.scalar.copy, 1)
        add(0, 2)
        quantise_wo(0, 0, early_scales[:, :P])
        weave(nc.scalar.copy, 2)
        x_fourth = placed([P, 2, P], BF16, "x_fourth", PAIRS_AT + 768)
        x_rows.append(x_fourth[:])
        nc.scalar.copy(x_fourth[:, 1, :], third_back[:, P:])
        quantise_x(0)
        quantise_wo(1, 1, early_scales[:, P:])
        quantise_x(1)
        add(0, 3)
        put_out([0], [chunks(0, 0)], 4, nc.scalar.copy)
        put_out([1], [chunks(0, 0)], 5, nc.scalar.copy)
        late_scales = placed([P, 2 * P], U8, "late_scales", PAIRS_AT + 512)
        quantise_wo(2, 2, late_scales[:, :P])
        quantise_wo(3, 3, late_scales[:, P:])
        put_out([0, 1], [chunks(1, 1)], 3, nc.scalar.copy)
        weave(nc.vector.tensor_copy, 3)
        put_out([2], [chunks(0, 1)], 2, nc.scalar.copy)
        put_out([3], [chunks(0, 1)], 0, nc.scalar.copy)
        quantise_x(2)
        quantise_x(3)
        put_out([0], [chunks(2, 2), chunks(3, 3)], 6, nc.vector.tensor_copy)
        put_out([1], [chunks(2, 2), chunks(3, 3)], 7, nc.scalar.copy)
        put_out([2], [chunks(2, 3)], 1, nc.vector.tensor_copy)
        put_out([3], [chunks(2, 3)], 4, nc.scalar.copy)
